import numpy as np, ml_dtypes
CORES = [6,15,38,47]
N = 4
import mx_ref
BF = ml_dtypes.bfloat16
def gcols(t, e):
    v = np.concatenate([t.reshape(8, 16, -1, 4), np.zeros((8, 16, 1, 4), BF)], axis=2)
    return np.ascontiguousarray(np.stack([v[g][:, e[g]] for g in range(8)])).reshape(128, -1)
def tile(rs):
    return np.stack(rs, axis=2).reshape(128, -1).astype(BF)
def cut(t, i, w=512):
    return t[:, w * i:w * i + w]
def pick(q, e):
    c = np.concatenate([q[0].reshape(128, -1, 4), np.zeros((128, 1, 4), np.uint8)], axis=1); s = np.concatenate([q[1], np.ones((16, 1), np.uint8)], axis=1)
    return (np.ascontiguousarray(c[:, e].reshape(128, -1)), np.ascontiguousarray(s[:, e]))
def join(*qs):
    return (np.concatenate([q[0] for q in qs], axis=1), np.concatenate([q[1] for q in qs], axis=1))
def put(q, e, v):
    c, s = q[0].reshape(128, -1, 4).copy(), q[1].copy(); c[:, e] = v[0].reshape(128, -1, 4); s[:, e] = v[1]
    return (c.reshape(128, -1), s)
def pk(c, s):
    return (np.ascontiguousarray(c), mx_ref.live(s))
def emit(q):
    return q[0], q[1]
def packed(v, rng):
    q = [mx_ref.quantize(np.ascontiguousarray(v[r])) for r in range(N)]
    return np.stack([a for a, b in q]), np.stack([mx_ref.plane(b, rng) for a, b in q])
def values_of_codes():
    e, c = np.zeros((128, 128, 4), np.float32), np.zeros((128, 2, 4), np.uint8)
    e[np.arange(128), np.arange(128), 0] = 1
    c[:127, :, 0] = np.arange(256).reshape(2, 128).T[:127]
    return mx_ref.matmul(mx_ref.quantize(e.reshape(128, 512).astype(BF)), (c.reshape(128, 8), np.full((16, 2), 127, np.uint8))).T.reshape(-1).astype(np.float64)
CODE_VALUE, SCALE_VALUE = values_of_codes(), 2.0 ** (np.arange(256) - 127.0)
def decode(q):
    return (CODE_VALUE[q[0]].reshape(16, 8, -1, 4) * SCALE_VALUE[q[1]][:, None, :, None] + 0.0).reshape(128, -1).astype(np.float32)
def f(rng, *shape):
    return mx_ref.flush((rng.standard_normal(shape, dtype=np.float32) * np.exp2(rng.integers(-2, 3, shape[:-1] + (1,)))).astype(BF))
def wide(rng, *shape, cols=0):
    v = rng.standard_normal(shape, dtype=np.float32) * np.exp2(rng.integers(-12, 13, shape)).astype(np.float32)
    if cols: v *= np.repeat(np.exp2(rng.integers(-cols, cols + 1, shape[:-2] + (1, shape[-1] // 4))) * (rng.random(shape[:-2] + (1, shape[-1] // 4)) > 0.0625), 4, axis=-1).astype(np.float32)
    return mx_ref.flush(v.astype(BF))
C, L, M, R = 320, 96, 224, 3
STEP = [1, 2, 1]
def order(p):
    return np.argsort(-(p[::16] + np.float32(0.0)), axis=1, kind="stable")
def numbers_of(rng):
    return {"x": np.array(f(rng, N, 128, 4 * C)), "u": np.array(f(rng, N, 128, 512)), "v": np.array(f(rng, N, 128, 512))}
def weights(rng, still=[]):
    w = np.array(f(rng, N, 128, 2048)).reshape(N, 8, 16, 4, 8, 16, 4)
    for i in still:
        w[:, :, i] = 0
        w[:, :, :, :, :, i] = 0
    c, p = packed(w.reshape(N, 128, 2048), rng)
    return {"wc": c, "ws": p}
def signs(rng):
    return np.stack([rng.permutation(8) % 2 * 2.0 - 1.0 for r in range(N)])
def setup_inputs(rng):
    return {**numbers_of(rng), **weights(rng)}
def setup_inputs_ties(rng):
    d = numbers_of(rng)
    e = rng.permutation(N)
    x = d["x"].reshape(N, 8, 16, C, 4)
    for r in range(N):
        k = np.zeros(C, int) if r == e[0] else rng.permutation(C) % 3
        a = x[r][:, :8, :3].copy()
        a[:, :, 2] = 0
        x[r][:, :8] = a[:, :, k]
    x[e[1]] = 0
    u = d["u"].reshape(N, 8, 16, 8, 16, 4)
    k = u.copy()
    u[:, :, :, :, :2] = 0
    for g in range(8): u[:, g, :8, g, :2] = k[:, g, :8, g, :2]
    return {"x": x.reshape(N, 128, 4 * C), "u": u.reshape(N, 128, 512), "v": d["v"], **weights(rng, range(8))}
def setup_inputs_near(rng):
    d = numbers_of(rng)
    x = d["x"].astype(np.float32).reshape(N, 8, 16, C, 4)
    s = np.arange(C) // 2
    g = ((s[:, None] >> np.arange(8)) & 1) * np.exp2(np.arange(8) - 23.0)
    x[:, :, 0] = 0
    x[:, :, 0, :, 0] = signs(rng)[:, :, None]
    for r in range(N):
        for i in rng.permutation(8)[:4]: x[r, i, 0, rng.integers(C), 0] *= np.float32(2.0 ** 30)
    x[:, :, 8] = g[:, :4]
    x[:, :, 9] = g[:, 4:]
    x[:, :, 10:] = rng.integers(4, 8, (N, 8, 6, C, 4)) * rng.choice([-1.0, 1.0], (N, 8, 6, C, 4)) * 2.0 ** -20
    u = d["u"].reshape(N, 128, 128, 4)
    k = np.where(rng.permutation(N) < N // 2, 2.0 ** -30, 1.0).astype(np.float32).astype(BF)
    u[:, :, ::16] = 0
    for h in range(0, 128, 16):
        u[:, h, h, 0] = k
        u[:, h + 8:h + 10, h] = k[:, None, None]
    return {"x": x.reshape(N, 128, 4 * C).astype(BF), "u": u.reshape(N, 128, 512), "v": d["v"], **weights(rng, [0, 8, 9, 10, 11, 12, 13, 14, 15])}
def setup_inputs_starts(rng):
    d = numbers_of(rng)
    x = d["x"].astype(np.float32).reshape(N, 8, 16, C, 4)
    u = d["u"].reshape(N, 128, 128, 4)
    size = np.where(rng.permutation(N) < N // 2, 2.0 ** -30, 1.0).astype(np.float32)
    x[:, :, :11] = 0
    n = np.stack([rng.permutation([0, 1, M // 2, M - 1, M, M + 1, C - 1, C]) for r in range(N)])
    o = np.argsort(rng.random((N, 8, C)), axis=2)
    for r in range(N):
        k = rng.permutation(8)
        for g in range(8):
            x[r, g, 0, :, 0] = np.where(rng.permutation(C) < n[r, g], 1, -rng.integers(0, 2, C)) * size[r]
            if r % 2 == 0:
                a, s = o[r, g], min(int(n[r, g]), M)
                seg, rest = rng.permutation(a[s:s + L]), np.concatenate([a[:s], a[s + L:]])
                if k[g] == 0: o[r ^ 1, g] = a
                if k[g] == 1: o[r ^ 1, g] = a[::-1]
                if k[g] == 2: o[r ^ 1, g] = np.concatenate([seg, rest])
                if k[g] == 3: o[r ^ 1, g] = np.concatenate([rest, seg])
    key = C - 1 - np.argsort(o, axis=2)
    z = ((key[:, :, :, None] >> np.arange(12)) & 1) * np.exp2(np.arange(12.0))
    for i in range(3): x[:, :, 8 + i] = z[:, :, :, 4 * i:4 * i + 4]
    k = size.astype(BF)
    u[:, :, ::16] = 0
    u[:, :, 1::16] = 0
    for h in range(0, 128, 16):
        u[:, h + 8:h + 11, h] = k[:, None, None]
        u[:, h, h + 1, 0] = k
    return {"x": x.reshape(N, 128, 4 * C).astype(BF), "u": u.reshape(N, 128, 512), "v": d["v"], **weights(rng, range(11))}
def setup_inputs_huge(rng):
    d = numbers_of(rng)
    x = 2.0 ** 30 * (0.8 + 0.2 * rng.random((N, 128, C, 4)))
    c = np.ones((N, C))
    half = int(rng.integers(2))
    for r in range(N):
        if 2 * r // N == half: c[r] = rng.permutation(C) % 2 * 2.0 - 1.0
    x *= c[:, None, :, None]
    u = d["u"].reshape(N, 128, 8, 16, 4)
    a = 2.0 ** 30 * (1 - 0.1 * rng.random((N, 128, 8, 2, 4))) * np.stack([signs(rng), signs(rng)], axis=2)[:, None, :, :, None]
    u[:, :, :, :2] = a.astype(np.float32).astype(BF)
    w = np.zeros((N, 128, 4, 128, 4), np.float32)
    i = np.arange(128)
    for b in range(4): w[:, i, b, i, b] = -1
    wc, ws = packed(w.reshape(N, 128, 2048).astype(BF), rng)
    return {"x": x.astype(np.float32).reshape(N, 128, 4 * C).astype(BF), "u": u.reshape(N, 128, 512), "v": d["v"], "wc": wc, "ws": ws}
def setup_inputs_spread(rng):
    d = setup_inputs(rng)
    d["x"] = wide(rng, N, 128, 4 * C, cols=6)
    return d
def check_inputs(d):
    b = []
    for k in ("x", "u", "v"):
        a = np.abs(d[k].astype(np.float32))
        if not (np.isfinite(a).all() and ((a == 0) | (a >= 2.0 ** -30) & (a <= 2.0 ** 30)).all()): b.append("a value of " + k)
    if ((d["wc"] & 0x7F) == 0x7F).any(): b.append("a code of wc that is no number")
    z = np.zeros((128, 4, 4), np.float32)
    z[:, 1] = 2.0 ** -30
    z[:, 2] = 2.0 ** 30
    c, s = emit(mx_ref.quantize(z.reshape(128, 16).astype(BF)))
    for r in range(N):
        p = mx_ref.live(d["ws"][r])
        if not ((p == s[0, 0]) | (p >= s[0, 1]) & (p <= s[0, 2])).all(): b.append("a scale of ws")
    return b
def reference(x, u, v, wc, ws):
    qu = [mx_ref.quantize(u[r]) for r in range(N)]
    lay = [pk(wc[r], ws[r]) for r in range(N)]
    now = [x[r] for r in range(N)]
    place = np.arange(C)
    for t in range(R):
        sent, o, start = [], [], []
        for r in range(N):
            q = mx_ref.quantize(now[r])
            p = mx_ref.matmul(qu[r], q)
            sent.append(q)
            o.append(order(p))
            start.append(np.minimum(np.sum(p[1::16] > 0, axis=1), M)[:, None])
        came = decode(join(*sent)).astype(BF)
        made, child = [], []
        for r in range(N):
            e = r ^ STEP[t]
            own = (place >= start[r]) & (place < start[r] + L)
            h = o[r].copy()
            for g in range(8): h[g, ~own[g]] = o[e][g][~np.isin(o[e][g], o[r][g][own[g]])]
            c = gcols(np.concatenate([now[r], cut(came, e, 4 * C)], axis=1), np.where(own, h, C + h))
            q = mx_ref.quantize(c)
            made.append(tile([mx_ref.matmul(pick(lay[r], np.arange(128 * b, 128 * b + 128)), q) * np.float32(0.015625) + c[:, b::4].astype(np.float32) for b in range(4)]))
            child.append(h)
        now = made
    y, ot = np.zeros((N, 128, C), np.float32), np.zeros((N, 8, C), np.float32)
    oc, osc = np.zeros((N, 128, 4 * C), np.uint8), np.zeros((N, 16, C), np.uint8)
    for r in range(N):
        q = mx_ref.quantize(now[r])
        y[r] = mx_ref.matmul(mx_ref.quantize(v[r]), q)
        ot[r] = child[r]
        oc[r], osc[r] = emit(q)
    return {"y": y, "ot": ot, "oc": oc, "osc": osc}

@@ -1,0 +1,339 @@
+from concourse.mybir import dt, AluOpType, ActivationFunctionType
+
+C, L, M, R = 320, 96, 224, 3
+STEP = [1, 2, 1]
+K = C // 16
+NV = 12
+ROW = C + 2
+HALF = ROW // 2
+MID = C // 2
+MARK = 576
+LIFT, DROP = 736, 1792
+
+SCRATCH = {
+    "X": ("sbuf", [128, 4 * C], "bfloat16"),
+    "U": ("sbuf", [128, 512], "bfloat16"),
+    "V": ("sbuf", [128, 512], "bfloat16"),
+    "UQ": ("sbuf", [128, 128], "float8_e4m3fn_x4"), "US": ("sbuf", [128, 128], "uint8"),
+    "UPQ": ("sbuf", [128, 256], "float8_e4m3fn_x4"), "UPS": ("sbuf", [128, 256], "uint8"),
+    "VQ": ("sbuf", [128, 128], "float8_e4m3fn_x4"), "VS": ("sbuf", [128, 128], "uint8"),
+    "WQ": ("sbuf", [128, 512], "float8_e4m3fn_x4"), "WS": ("sbuf", [128, 512], "uint8"),
+    "EB": ("sbuf", [128, 516], "bfloat16"), "E1": ("sbuf", [128, 516], "bfloat16"),
+    "EQ": ("sbuf", [128, 512], "float8_e4m3fn_x4"), "ES": ("sbuf", [128, 512], "uint8"),
+    "FQ": ("sbuf", [128, C], "float8_e4m3fn_x4"), "FS": ("sbuf", [128, C], "uint8"),
+    "PI": ("sbuf", [128, 2], "int32"), "PA": ("sbuf", [128, 2], "int32"), "PM": ("sbuf", [128, 2], "float32"),
+    "T16": ("sbuf", [128, C], "bfloat16"),
+    "UOI": ("sbuf", [128, 16], "int32"), "UO": ("sbuf", [128, 16], "uint16"),
+    "JB": ("sbuf", [128, C], "bfloat16"),
+    "C2": ("sbuf", [128, C + K], "float32"),
+    "KI": ("sbuf", [128, K], "float32"), "QW": ("sbuf", [128, K], "float32"),
+    "MASK": ("sbuf", [128, C], "bfloat16"), "KEEP": ("sbuf", [128, C], "bfloat16"),
+    "CA": ("sbuf", [128, C], "bfloat16"), "CB": ("sbuf", [128, C], "bfloat16"),
+    "C0": ("sbuf", [128, C], "bfloat16"), "CH": ("sbuf", [128, C], "bfloat16"), "CZ": ("sbuf", [128, C], "float16"),
+    "RP": ("sbuf", [128, 8], "float32"),
+    "MX": ("sbuf", [128, C], "float32"), "FW": ("sbuf", [128, C], "float32"),
+    "EQF": ("sbuf", [128, C], "bfloat16"), "COR": ("sbuf", [128, C], "bfloat16"),
+    "FL": ("sbuf", [128, K * ROW], "bfloat16"), "JK": ("sbuf", [128, (K - NV) * ROW], "bfloat16"),
+    "CS": ("sbuf", [128, 2 + NV * HALF], "float16"),
+    "AC": ("sbuf", [128, 2 * K], "float32"), "WR": ("sbuf", [128, K], "float32"),
+    "NS": ("sbuf", [128, C], "bfloat16"), "NJ": ("sbuf", [128, C], "bfloat16"), "SM": ("sbuf", [128, 4], "float32"),
+    "AB": ("sbuf", [128, C + K], "float32"), "SG": ("sbuf", [128, C + K], "bfloat16"), "TAB": ("sbuf", [128, C], "bfloat16"),
+    "ZJ": ("sbuf", [128, C], "bfloat16"), "ZQ": ("sbuf", [128, C], "bfloat16"), "FG": ("sbuf", [128, C], "bfloat16"),
+    "CU": ("sbuf", [128, C], "float16"), "VZ": ("sbuf", [128, C], "float16"), "VC": ("sbuf", [128, C], "float16"),
+    "VH": ("sbuf", [128, C], "float16"),
+    "T1": ("sbuf", [128, K], "float32"), "T2": ("sbuf", [128, K], "float32"), "T3": ("sbuf", [128, K], "float32"),
+    "POS": ("sbuf", [128, K], "uint16"), "OFF": ("sbuf", [128, K], "uint16"),
+    "H": ("sbuf", [128, 2 * C], "bfloat16"),
+    "WIN": ("sbuf", [128, 8 * C], "bfloat16"), "F": ("sbuf", [128, 4 * C], "bfloat16"), "F64": ("sbuf", [128, 4 * C], "bfloat16"),
+    "TT": ("sbuf", [128, 4 * C], "bfloat16"),
+    "OT": ("sbuf", [128, C], "float32"), "Y": ("sbuf", [128, C], "float32"),
+}
+for _t in range(R + 1):
+    SCRATCH["TQ%d" % _t] = ("sbuf", [128, C], "float8_e4m3fn_x4")
+    SCRATCH["TS%d" % _t] = ("sbuf", [128, C], "uint8")
+for _t in range(R):
+    SCRATCH["LQ%d" % _t] = ("sbuf", [128, C], "float8_e4m3fn_x4")
+    SCRATCH["LS%d" % _t] = ("sbuf", [128, C], "uint8")
+    SCRATCH["RK%d" % _t] = ("sbuf", [128, K], "uint16")
+    SCRATCH["LR%d" % _t] = ("sbuf", [128, K], "uint16")
+for _t in range(8):
+    SCRATCH["B%d" % _t] = ("psum", [128, 512], "float32")
+
+NDMA = 14
+SEMAPHORES = ["cv", "cs", "ct", "cg", "sent"] + ["d%d" % i for i in range(NDMA)] + ["aq%d" % t for t in range(R)] + ["ar%d" % t for t in range(R)]
+
+
+def rank_program(g, core, T, topo):
+    rank = T.rank_of(core)
+    if rank is None:
+        return
+    A, F_ = AluOpType, ActivationFunctionType
+    queue = {"v": g.vector, "s": g.scalar, "t": g.tensor, "g": g, "y": g.sync}
+    count = {"cv": 0, "cs": 0, "ct": 0, "cg": 0, "sent": 0}
+    known = {q: {} for q in queue}
+    writer, readers = {}, {}
+    ndma = [0]
+
+    def settle(q, events):
+        need = {}
+        for s, n, kn in events:
+            if known[q].get(s, 0) < n and need.get(s, (0, None))[0] < n:
+                need[s] = (n, kn)
+        for s in list(need):
+            n = need[s][0]
+            if any(o != s and need[o][1].get(s, 0) >= n for o in need):
+                del need[s]
+        for s, (n, kn) in need.items():
+            queue[q].wait_ge(T.sem[s], n)
+            known[q][s] = n
+            for a, b in kn.items():
+                if known[q].get(a, 0) < b:
+                    known[q][a] = b
+
+    def order(q, reads, writes):
+        ev = [writer[k] for k in reads if k in writer]
+        for k in writes:
+            if k in writer:
+                ev.append(writer[k])
+            ev.extend(readers.get(k, []))
+        settle(q, ev)
+
+    def note(e, reads, writes):
+        for k in reads:
+            readers.setdefault(k, []).append(e)
+        for k in writes:
+            writer[k] = e
+            readers[k] = []
+
+    def op(q, call, reads, writes):
+        order(q, reads, writes)
+        s = "c" + q
+        call().then_inc(T.sem[s], 1)
+        count[s] += 1
+        note((s, count[s], dict(known[q])), reads, writes)
+
+    def dma(q, out, in_, reads, writes):
+        order(q, reads, writes)
+        s = "d%d" % ndma[0]
+        ndma[0] += 1
+        queue[q].dma_start(out, in_).then_inc(T.sem[s], 16)
+        count[s] = 16
+        note((s, 16, dict(known[q])), reads, writes)
+
+    def send(out, in_, sem, dst, reads):
+        order("g", reads, [])
+        rid, pid, _ = topo.addr(dst)
+        g.remote_dma(out, in_, T.sem[sem], T.sem.sent, pid, rid, topo.mask(core, dst))
+        count["sent"] += len(topo.engines(core, dst))
+
+    V, S, P = g.vector, g.scalar, g.tensor
+
+    def ts(out, in0, s1, s2, op0, op1, reads, writes):
+        if op1 is None:
+            op("v", lambda: V.tensor_scalar(out, in0, s1, None, op0), reads, writes)
+        else:
+            op("v", lambda: V.tensor_scalar(out, in0, s1, s2, op0, op1), reads, writes)
+
+    def tt(out, in0, in1, o, reads, writes):
+        op("v", lambda: V.tensor_tensor(out, in0, in1, o), reads, writes)
+
+    def cp(out, in_, reads, writes):
+        op("v", lambda: V.tensor_copy(out, in_), reads, writes)
+
+    def scan(out, d0, d1, init, op0, op1, reads, writes):
+        op("v", lambda: V.tensor_tensor_scan(out, d0, d1, init, op0, op1), reads, writes)
+
+    def fill(ap, c, writes):
+        op("v", lambda: V.memset(ap, c), [], writes)
+
+    def quant(q, s, in_, reads, writes):
+        op("v", lambda: V.quantize_mx(q, s, in_), reads, writes)
+
+    def act(out, in_, f, reads, writes, **kw):
+        op("s", lambda: S.activation(out, in_, f, **kw), reads, writes)
+
+    def mm(bank, lq, ls, rq, rs, reads):
+        op("t", lambda: P.matmul_mx(T[bank][:, 0:C], lq, ls, rq, rs, True, True), reads, [bank])
+
+    def iota(out, pattern, base, cm, writes, small=True):
+        if small:
+            op("g", lambda: g.iota(out, pattern, base, cm, allow_small_or_imprecise_dtypes=True), [], writes)
+        else:
+            op("g", lambda: g.iota(out, pattern, base, cm), [], writes)
+
+    u8, u32 = dt.uint8, dt.uint32
+    end16 = slice(15, C, 16)
+
+    dma("y", T.U[:], T.u[:], [], ["U"])
+    dma("s", T.X[:], T.x[:], [], ["X"])
+    iota(T.PI[:], [[15, 2]], 0, 1, ["PI"], False)
+    iota(T.UOI[:], [[1, 2], [16, 8]], 0, 0, ["UOI"], False)
+    iota(T.T16[:], [[0, K], [1, 16]], 0, 0, ["T16"])
+    iota(T.KI[:], [[16, K]], 0, 0, ["KI"])
+    iota(T.JB[:], [[1, C]], -MID, 0, ["JB"])
+    iota(T.C2[:, 0:C], [[2, C]], -(2 * M + L - 1), 0, ["C2r"])
+    fill(T.E1[:], 1.0, ["E1"])
+    fill(T.CS[:, 0:2], 0.0, ["CS0"])
+    fill(T.FL[:, ROW - 1:NV * ROW:ROW], 0.0, ["FLc"])
+    fill(T.AC[:, 2 * K - 1:2 * K], float(C - MID), ["a2_%d" % (K - 1)])
+    ts(T.PA[:], T.PI[:], 15, None, A.bitwise_and, None, ["PI"], ["PA"])
+    cp(T.UO[:], T.UOI[:], ["UOI"], ["UO"])
+    cp(T.PM[:], T.PA[:], ["PA"], ["PM"])
+    pm, pm1 = T.PM[:, 0:1], T.PM[:, 1:2]
+    ts(T.MASK[:], T.T16[:], pm, None, A.is_equal, None, ["T16", "PM"], ["MASK"])
+    ts(T.KEEP[:], T.T16[:], pm, None, A.not_equal, None, ["T16", "PM"], ["KEEP"])
+    ts(T.FL[:, (NV + 1) * ROW - 1:(K - 1) * ROW:ROW], T.KI[:, NV:K - 1], -1.0, float(MID - 16), A.mult, A.add, ["KI"], ["FLs"])
+    ts(T.RP[:, 0:1], pm, 0.0, -float(DROP), A.is_equal, A.mult, ["PM"], ["RP0"])
+    quant(T.UQ[:], T.US[:], T.U[:], ["U"], ["UQ", "US"])
+    cp(T.UPQ[:].bitcast(u32), T.UQ[:].bitcast(u32).indirect(T.UO[:]), ["UQ", "UO"], ["UPQ"])
+    act(T.UPS[:], T.US[:].indirect(T.UO[:]), F_.Copy, ["US", "UO"], ["UPS"])
+    quant(T.TQ0[:], T.TS0[:], T.X[:], ["X"], ["TQ0"])
+    order("y", ["X"], [])
+    dma("y", T.WQ[:].bitcast(u8), T.wc[:], [], ["WQ"])
+    dma("y", T.WS[:], T.ws[:], [], ["WS"])
+    dma("y", T.V[:], T.v[:], [], ["V"])
+    thr_b, pos_b, off_b, ch_b = T.RP[:, 1:2], T.RP[:, 2:3], T.RP[:, 3:4], T.RP[:, 4:5]
+    base = LIFT - MARK
+
+    for t in range(R):
+        dst = T.cores[rank ^ STEP[t]]
+        ne = len(topo.engines(dst, core))
+        tq, tsc, lq, lsc = T["TQ%d" % t], T["TS%d" % t], T["LQ%d" % t], T["LS%d" % t]
+        rk, lr = T["RK%d" % t], T["LR%d" % t]
+        kq = "TQ%d" % t
+        writer["LQ%d" % t] = ("aq%d" % t, 2 * ne, {})
+        writer["LR%d" % t] = ("ar%d" % t, ne, {})
+
+        mm("B0", T.UPQ[:, 0:128], T.UPS[:, 0:128], tq[:], tsc[:], ["UPQ", "UPS", kq])
+        mm("B2", T.UPQ[:, 128:256], T.UPS[:, 128:256], tq[:], tsc[:], ["UPQ", "UPS", kq])
+        mm("B1", T.UPQ[:, 0:128], T.UPS[:, 0:128], tq[:], tsc[:], ["UPQ", "UPS", kq])
+        send(lq[:].bitcast(u8), tq[:].bitcast(u8), "aq%d" % t, dst, [kq])
+        send(lsc[:], tsc[:], "aq%d" % t, dst, [kq])
+        if t == 0:
+            op("g", lambda: g.affine_select(T.EB[:], T.E1[:], [[1, 516]], A.is_equal, 0.0, -3, -4), ["E1"], ["EB"])
+        av, asc = T.B0, T.B1
+        tt(T.MX[:], av[:, 0:C], T.MASK[:], A.mult, ["B0", "MASK"], ["MX"])
+        act(T.NS[:], T.B2[:, 0:C], F_.Sign, ["B2"], ["NS"])
+        scan(T.FW[:], T.KEEP[:], T.MX[:], 0.0, A.mult, A.add, ["KEEP", "MX"], ["FW"])
+        act(T.NJ[:], T.NS[:], F_.Relu, ["NS"], ["NJ", "n"], accum_out=T.SM[:, 0:1])
+        tt(T.EQF[:], av[:, 0:C], T.FW[:], A.is_equal, ["B0", "FW"], ["EQF"])
+
+        def vcount(k):
+            e, o, sc = 16 * k + 16, k * ROW + 1, T.FW[:, 16 * k + 15:16 * k + 16]
+            ts(T.FL[:, o:o + e], av[:, 0:e], sc, 0.5, A.is_lt, A.subtract, ["B0", "FW"], ["fa%d" % k])
+            ts(T.FL[:, o + e:o + C], av[:, e:C], sc, 0.5, A.is_le, A.subtract, ["B0", "FW"], ["fb%d" % k])
+
+        def ssign(k):
+            o = k * ROW + 1
+            act(T.FL[:, o:o + C], asc[:, 0:C], F_.Sign, ["B1", "FW"], ["fa%d" % k], bias=T.FW[:, 16 * k + 15:16 * k + 16], scale=-1.0)
+
+        def scount(k):
+            e, o, j = 16 * k + 16, k * ROW, (k - NV) * ROW
+            act(T.JK[:, j:j + e + 1], T.FL[:, o:o + e + 1], F_.Relu, ["fa%d" % k, "FL0"], ["ja%d" % k, "a1_%d" % k], accum_out=T.AC[:, k:k + 1])
+            if k < K - 1:
+                act(T.JK[:, j + e + 1:j + ROW], T.FL[:, o + e + 1:o + ROW], F_.Relu, ["fa%d" % k, "FLs"], ["jb%d" % k, "a2_%d" % k],
+                    scale=-1.0, accum_out=T.AC[:, K + k:K + k + 1])
+
+        vcount(0)
+        scan(T.COR[:], T.KEEP[:], T.EQF[:], 0.0, A.mult, A.add, ["KEEP", "EQF"], ["COR"])
+        vcount(1)
+        cp(T.FL[:, 0:K * ROW:ROW], T.COR[:, end16], ["COR"], ["FL0"])
+        ssign(NV)
+        act(T.SM[:, 1:2], T.SM[:, 0:1], F_.Relu, ["n"], ["x2"], bias=float(2 * M), scale=-2.0)
+        for k in range(NV, K):
+            if k + 1 < K:
+                ssign(k + 1)
+            scount(k)
+        for k in range(2, NV):
+            vcount(k)
+        scan(T.CS[:, 2:2 + NV * HALF], T.FL[:, 0:NV * ROW:2], T.FL[:, 1:NV * ROW:2], 0.0, A.add, A.add,
+             ["FL0", "FLc"] + ["fa%d" % k for k in range(NV)] + ["fb%d" % k for k in range(NV)], ["CS"])
+        tt(T.WR[:, NV:K], T.AC[:, K + NV:2 * K], T.AC[:, NV:K], A.subtract,
+           ["a1_%d" % k for k in range(NV, K)] + ["a2_%d" % k for k in range(NV, K)], ["WRs"])
+        tt(T.WR[:, 0:NV], T.CS[:, 1:1 + NV * HALF:HALF], T.CS[:, 1 + HALF:2 + NV * HALF:HALF], A.subtract, ["CS", "CS0"], ["WRv"])
+        ts(rk[:], T.WR[:], float(MID), None, A.add, None, ["WRs", "WRv"], ["RK%d" % t])
+        send(lr[:], rk[:], "ar%d" % t, dst, ["RK%d" % t])
+
+        if t == 0:
+            ts(T.QW[:], T.KI[:], pm, None, A.add, None, ["KI", "PM"], ["QW"])
+            for b in range(4):
+                quant(T.EQ[:, 128 * b:128 * b + 128], T.ES[:, 128 * b:128 * b + 128], T.EB[:, 3 - b:515 - b], ["EB"], ["EQ%d" % b])
+            ts(T.C2[:, C:C + K], T.QW[:], 2.0, -float(2 * M + L - 1), A.mult, A.add, ["QW"], ["C2w"])
+            ts(T.CA[:], T.T16[:], pm, float(LIFT), A.is_equal, A.mult, ["T16", "PM"], ["CA"])
+            ts(T.CB[:], T.T16[:], pm1, -float(DROP), A.is_equal, A.mult, ["T16", "PM"], ["CB"])
+        act(T.AB[:], T.C2[:], F_.Abs, ["C2r", "C2w", "x2"], ["AB"], bias=T.SM[:, 1:2])
+        if t == 0:
+            act(thr_b, T.RP[:, 0:1], F_.Identity, ["RP0"], ["RP1"], bias=float(M + C + base))
+            act(pos_b, T.RP[:, 0:1], F_.Identity, ["RP0"], ["RP2"], bias=float(base))
+            act(off_b, T.RP[:, 0:1], F_.Identity, ["RP0"], ["RP3"], bias=float(LIFT - MID))
+        else:
+            act(T.SM[:, 2:3], T.SM[:, 1:2], F_.Identity, ["x2", "RP1"], ["thr"], bias=thr_b, scale=-0.5)
+        act(T.SG[:], T.AB[:], F_.Sign, ["AB"], ["SG"], bias=-float(L))
+        if t == 0:
+            act(T.SM[:, 2:3], T.SM[:, 1:2], F_.Identity, ["x2", "RP1"], ["thr"], bias=thr_b, scale=-0.5)
+        act(T.TAB[:], T.SG[:, 0:C], F_.Copy, ["SG"], ["TAB"], scale=float(MARK))
+        for b in range(4):
+            mm("B%d" % (4 + b), T.EQ[:, 128 * b:128 * b + 128], T.ES[:, 128 * b:128 * b + 128], lq[:], lsc[:], ["EQ%d" % b, "LQ%d" % t])
+        cp(T.H[:, C:2 * C].indirect(rk[:]), T.JB[:], ["JB", "RK%d" % t], ["H"])
+        if t == 0:
+            tt(T.C0[:], T.CA[:], T.CB[:], A.add, ["CA", "CB"], ["C0"])
+        tt(T.ZJ[:], T.TAB[:].indirect(rk[:]), T.JB[:], A.min, ["TAB", "JB", "RK%d" % t], ["ZJ"])
+        if t == 0:
+            cp(T.CZ[:], T.C0[:], ["C0"], ["CZ"])
+            act(T.CH[:], T.C0[:], F_.Copy, ["C0"], ["CH"])
+            act(ch_b, T.C0[:, 15:16], F_.Identity, ["C0"], ["RP4"], bias=float(C // 2))
+            tt(T.CZ[:, end16], T.C0[:, end16], T.QW[:], A.add, ["C0", "QW"], ["CZ"])
+        act(T.CH[:, end16], T.SG[:, C:C + K], F_.Identity, ["SG", "RP4"], ["CH"], bias=ch_b, scale=float(C // 2))
+        for b in range(4):
+            act(T.WIN[:, (2 * b + 1) * C:(2 * b + 2) * C], T["B%d" % (4 + b)][:, 0:C], F_.Copy, ["B%d" % (4 + b)], ["WD%d" % b], scale=64.0)
+        if t == 0:
+            for b in range(4):
+                act(T.WIN[:, 2 * b * C:(2 * b + 1) * C], T.X[:, b:4 * C:4], F_.Copy, ["X"], ["WT%d" % b], scale=64.0)
+
+        cp(T.ZQ[:].indirect(lr[:]), T.ZJ[:], ["ZJ", "LR%d" % t], ["ZQ"])
+        ts(T.FG[:], T.ZQ[:], -float(MARK // 2), None, A.is_gt, None, ["ZQ"], ["FG"])
+        scan(T.VZ[:], T.ZQ[:], T.CZ[:], -4096.0, A.max, A.add, ["ZQ", "CZ"], ["VZ"])
+        scan(T.CU[:], T.FG[:], T.MASK[:], float(C - 1 - MARK), A.add, A.min, ["FG", "MASK"], ["CU"])
+        scan(T.VC[:], T.CU[:], T.C0[:], -4096.0, A.max, A.add, ["CU", "C0"], ["VC"])
+        ts(T.T1[:], T.VC[:, end16], T.SM[:, 2:3], float(L), A.is_ge, A.mult, ["VC", "thr"], ["T1"])
+        tt(T.T2[:], T.T1[:], T.VC[:, end16], A.add, ["T1", "VC"], ["T2"])
+        tt(T.T3[:], T.T2[:], T.VZ[:, end16], A.min, ["T2", "VZ"], ["T3"])
+        ts(T.POS[:], T.T3[:], pos_b, None, A.subtract, None, ["T3", "RP2"], ["POS"])
+        cp(T.H[:].indirect(T.POS[:]), T.ZQ[:], ["ZQ", "POS"], ["H"])
+        scan(T.VH[:], T.H[:, C:2 * C], T.CH[:], -4096.0, A.max, A.add, ["H", "CH"], ["VH"])
+        if t == R - 1:
+            act(T.OT[:], T.H[:, C:2 * C], F_.Identity, ["H"], ["OT"], bias=float(MID))
+            dma("y", T.ot[:], T.OT[0:128:16, :], ["OT"], [])
+        ts(T.OFF[:], T.VH[:, end16], off_b, None, A.subtract, None, ["VH", "RP3"], ["OFF"])
+
+        for b in range(2):
+            ts(T.F[:, b:4 * C:4], T.WIN[:, 2 * b * C:(2 * b + 2) * C].indirect(T.OFF[:]), 0.015625, None, A.mult, None,
+               ["WT%d" % b, "WD%d" % b, "OFF"], ["F%d" % b])
+        for b in range(2, 4):
+            act(T.F[:, b:4 * C:4], T.WIN[:, 2 * b * C:(2 * b + 2) * C].indirect(T.OFF[:]), F_.Copy,
+                ["WT%d" % b, "WD%d" % b, "OFF"], ["F%d" % b], scale=0.015625)
+        quant(T.FQ[:], T.FS[:], T.F[:], ["F%d" % b for b in range(4)], ["FQ"])
+        for b in range(4):
+            act(T.F64[:, b * C:(b + 1) * C], T.F[:, b:4 * C:4], F_.Copy, ["F%d" % b], ["G%d" % b], scale=64.0)
+        for b in range(4):
+            mm("B%d" % b, T.WQ[:, 128 * b:128 * b + 128], T.WS[:, 128 * b:128 * b + 128], T.FQ[:], T.FS[:], ["WQ", "WS", "FQ"])
+        if t == 0:
+            quant(T.VQ[:], T.VS[:], T.V[:], ["V"], ["VQ"])
+        for b in range(4):
+            tt(T.WIN[:, 2 * b * C:(2 * b + 1) * C], T["B%d" % b][:, 0:C], T.F64[:, b * C:(b + 1) * C], A.add, ["B%d" % b, "G%d" % b], ["WT%d" % b])
+        for b in range(2):
+            act(T.TT[:, b:4 * C:4], T.WIN[:, 2 * b * C:(2 * b + 1) * C], F_.Copy, ["WT%d" % b], ["TT%d" % b], scale=0.015625)
+        for b in range(2, 4):
+            ts(T.TT[:, b:4 * C:4], T.WIN[:, 2 * b * C:(2 * b + 1) * C], 0.015625, None, A.mult, None, ["WT%d" % b], ["TT%d" % b])
+        quant(T["TQ%d" % (t + 1)][:], T["TS%d" % (t + 1)][:], T.TT[:], ["TT%d" % b for b in range(4)], ["TQ%d" % (t + 1)])
+
+    tq, tsc, kq = T["TQ%d" % R], T["TS%d" % R], "TQ%d" % R
+    mm("B4", T.VQ[:], T.VS[:], tq[:], tsc[:], ["VQ", kq])
+    dma("s", T.oc[:], tq[:].bitcast(u8), [kq], [])
+    for k in range(4):
+        dma("y" if k < 2 else "s", T.osc[4 * k:4 * k + 4, :], tsc[32 * k:32 * k + 4, :], [kq], [])
+    cp(T.Y[:], T.B4[:, 0:C], ["B4"], ["Y"])
+    dma("y", T.y[:], T.Y[:], ["Y"], [])
+    for s, n in count.items():
+        if known["g"].get(s, 0) < n:
+            g.wait_ge(T.sem[s], n)

@@ -3,64 +3,30 @@ from concourse.mybir import dt, AluOpType, ActivationFunctionType
 C, L, M, R = 320, 96, 224, 3
 STEP = [1, 2, 1]
 K = C // 16
-NV = 12
+KV, KE, KS = 9, 12, 16
 ROW = C + 2
 HALF = ROW // 2
 MID = C // 2
 MARK = 576
 LIFT, DROP = 736, 1792
+BF, F32, F16, Q4, U8, U16, I32 = "bfloat16", "float32", "float16", "float8_e4m3fn_x4", "uint8", "uint16", "int32"
 
-SCRATCH = {
-    "X": ("sbuf", [128, 4 * C], "bfloat16"),
-    "U": ("sbuf", [128, 512], "bfloat16"),
-    "V": ("sbuf", [128, 512], "bfloat16"),
-    "UQ": ("sbuf", [128, 128], "float8_e4m3fn_x4"), "US": ("sbuf", [128, 128], "uint8"),
-    "UPQ": ("sbuf", [128, 256], "float8_e4m3fn_x4"), "UPS": ("sbuf", [128, 256], "uint8"),
-    "VQ": ("sbuf", [128, 128], "float8_e4m3fn_x4"), "VS": ("sbuf", [128, 128], "uint8"),
-    "WQ": ("sbuf", [128, 512], "float8_e4m3fn_x4"), "WS": ("sbuf", [128, 512], "uint8"),
-    "EB": ("sbuf", [128, 516], "bfloat16"), "E1": ("sbuf", [128, 516], "bfloat16"),
-    "EQ": ("sbuf", [128, 512], "float8_e4m3fn_x4"), "ES": ("sbuf", [128, 512], "uint8"),
-    "FQ": ("sbuf", [128, C], "float8_e4m3fn_x4"), "FS": ("sbuf", [128, C], "uint8"),
-    "PI": ("sbuf", [128, 2], "int32"), "PA": ("sbuf", [128, 2], "int32"), "PM": ("sbuf", [128, 2], "float32"),
-    "T16": ("sbuf", [128, C], "bfloat16"),
-    "UOI": ("sbuf", [128, 16], "int32"), "UO": ("sbuf", [128, 16], "uint16"),
-    "JB": ("sbuf", [128, C], "bfloat16"),
-    "C2": ("sbuf", [128, C + K], "float32"),
-    "KI": ("sbuf", [128, K], "float32"), "QW": ("sbuf", [128, K], "float32"),
-    "MASK": ("sbuf", [128, C], "bfloat16"), "KEEP": ("sbuf", [128, C], "bfloat16"),
-    "CA": ("sbuf", [128, C], "bfloat16"), "CB": ("sbuf", [128, C], "bfloat16"),
-    "C0": ("sbuf", [128, C], "bfloat16"), "CH": ("sbuf", [128, C], "bfloat16"), "CZ": ("sbuf", [128, C], "float16"),
-    "RP": ("sbuf", [128, 8], "float32"),
-    "MX": ("sbuf", [128, C], "float32"), "FW": ("sbuf", [128, C], "float32"),
-    "EQF": ("sbuf", [128, C], "bfloat16"), "COR": ("sbuf", [128, C], "bfloat16"),
-    "FL": ("sbuf", [128, K * ROW], "bfloat16"), "JK": ("sbuf", [128, (K - NV) * ROW], "bfloat16"),
-    "CS": ("sbuf", [128, 2 + NV * HALF], "float16"),
-    "AC": ("sbuf", [128, 2 * K], "float32"), "WR": ("sbuf", [128, K], "float32"),
-    "NS": ("sbuf", [128, C], "bfloat16"), "NJ": ("sbuf", [128, C], "bfloat16"), "SM": ("sbuf", [128, 4], "float32"),
-    "AB": ("sbuf", [128, C + K], "float32"), "SG": ("sbuf", [128, C + K], "bfloat16"), "TAB": ("sbuf", [128, C], "bfloat16"),
-    "ZJ": ("sbuf", [128, C], "bfloat16"), "ZQ": ("sbuf", [128, C], "bfloat16"), "FG": ("sbuf", [128, C], "bfloat16"),
-    "CU": ("sbuf", [128, C], "float16"), "VZ": ("sbuf", [128, C], "float16"), "VC": ("sbuf", [128, C], "float16"),
-    "VH": ("sbuf", [128, C], "float16"),
-    "T1": ("sbuf", [128, K], "float32"), "T2": ("sbuf", [128, K], "float32"), "T3": ("sbuf", [128, K], "float32"),
-    "POS": ("sbuf", [128, K], "uint16"), "OFF": ("sbuf", [128, K], "uint16"),
-    "H": ("sbuf", [128, 2 * C], "bfloat16"),
-    "WIN": ("sbuf", [128, 8 * C], "bfloat16"), "F": ("sbuf", [128, 4 * C], "bfloat16"), "F64": ("sbuf", [128, 4 * C], "bfloat16"),
-    "TT": ("sbuf", [128, 4 * C], "bfloat16"),
-    "OT": ("sbuf", [128, C], "float32"), "Y": ("sbuf", [128, C], "float32"),
-}
-for _t in range(R + 1):
-    SCRATCH["TQ%d" % _t] = ("sbuf", [128, C], "float8_e4m3fn_x4")
-    SCRATCH["TS%d" % _t] = ("sbuf", [128, C], "uint8")
-for _t in range(R):
-    SCRATCH["LQ%d" % _t] = ("sbuf", [128, C], "float8_e4m3fn_x4")
-    SCRATCH["LS%d" % _t] = ("sbuf", [128, C], "uint8")
-    SCRATCH["RK%d" % _t] = ("sbuf", [128, K], "uint16")
-    SCRATCH["LR%d" % _t] = ("sbuf", [128, K], "uint16")
+SCRATCH = {}
+for _names, _n, _d in (
+        ("X F F64 TT", 4 * C, BF), ("U V", 512, BF), ("UQ VQ", 128, Q4), ("US VS", 128, U8), ("UPQ", 256, Q4), ("UPS", 256, U8),
+        ("WQ EQ", 512, Q4), ("WS ES", 512, U8), ("EB E1", 516, BF), ("FQ TQ0 TQ1 TQ2 TQ3 LQ0 LQ1 LQ2", C, Q4),
+        ("FS TS0 TS1 TS2 TS3 LS0 LS1 LS2", C, U8), ("PI PA", 2, I32), ("PM", 2, F32), ("UOI", 16, I32), ("UO", 16, U16),
+        ("T16 JB MASK KEEP CA CB C0 CH EQF COR NS NJ TAB ZJ ZQ FG", C, BF), ("CZ CU VZ VC VH", C, F16), ("C2 AB", C + K, F32),
+        ("SG", C + K, BF), ("KI QW T1 T2 T3", K, F32), ("RP", 8, F32), ("MX FW OT Y", C, F32), ("FL JK", K * ROW, BF),
+        ("CS", 2 + KV * HALF, F16), ("CL", (K - KE) * HALF, F16), ("AC", 2 * K, F32), ("WR", KE, F32), ("SM", 4, F32),
+        ("POS OFF RK0 RK1 RK2", K, U16), ("LA0 LA1 LA2", KE, U16), ("LB0 LB1 LB2", K - KE, U16), ("H", 2 * C, BF), ("WIN", 8 * C, BF)):
+    for _x in _names.split():
+        SCRATCH[_x] = ("sbuf", [128, _n], _d)
 for _t in range(8):
-    SCRATCH["B%d" % _t] = ("psum", [128, 512], "float32")
+    SCRATCH["B%d" % _t] = ("psum", [128, 512], F32)
 
-NDMA = 14
-SEMAPHORES = ["cv", "cs", "ct", "cg", "sent"] + ["d%d" % i for i in range(NDMA)] + ["aq%d" % t for t in range(R)] + ["ar%d" % t for t in range(R)]
+SEMAPHORES = (["cv", "cs", "ct", "cg", "sent"] + ["d%d" % i for i in range(16)]
+              + ["%s%d" % (a, t) for a in ("aq", "aa", "ab") for t in range(R)])
 
 
 def rank_program(g, core, T, topo):
@@ -152,8 +118,8 @@ def rank_program(g, core, T, topo):
     def act(out, in_, f, reads, writes, **kw):
         op("s", lambda: S.activation(out, in_, f, **kw), reads, writes)
 
-    def mm(bank, lq, ls, rq, rs, reads):
-        op("t", lambda: P.matmul_mx(T[bank][:, 0:C], lq, ls, rq, rs, True, True), reads, [bank])
+    def mm(bank, lq, ls, rq, rs, reads, n=C):
+        op("t", lambda: P.matmul_mx(T[bank][:, 0:n], lq, ls, rq, rs, True, True), reads, [bank])
 
     def iota(out, pattern, base, cm, writes, small=True):
         if small:
@@ -161,149 +127,190 @@ def rank_program(g, core, T, topo):
         else:
             op("g", lambda: g.iota(out, pattern, base, cm), [], writes)
 
+    def quant_state(t, tile, reads):
+        for h in range(2):
+            quant(T["TQ%d" % t][:, h * MID:(h + 1) * MID], T["TS%d" % t][:, h * MID:(h + 1) * MID], tile[:, 4 * h * MID:4 * (h + 1) * MID],
+                  reads[h], ["TQ%d_%d" % (t, h)])
+
     u8, u32 = dt.uint8, dt.uint32
     end16 = slice(15, C, 16)
 
     dma("y", T.U[:], T.u[:], [], ["U"])
-    dma("s", T.X[:], T.x[:], [], ["X"])
+    dma("y", T.X[:, 0:2 * C], T.x[:, 0:2 * C], [], ["X0"])
+    dma("y", T.X[:, 2 * C:4 * C], T.x[:, 2 * C:4 * C], [], ["X1"])
     iota(T.PI[:], [[15, 2]], 0, 1, ["PI"], False)
     iota(T.UOI[:], [[1, 2], [16, 8]], 0, 0, ["UOI"], False)
     iota(T.T16[:], [[0, K], [1, 16]], 0, 0, ["T16"])
     iota(T.KI[:], [[16, K]], 0, 0, ["KI"])
-    iota(T.JB[:], [[1, C]], -MID, 0, ["JB"])
     iota(T.C2[:, 0:C], [[2, C]], -(2 * M + L - 1), 0, ["C2r"])
     fill(T.E1[:], 1.0, ["E1"])
+    op("g", lambda: g.affine_select(T.EB[:], T.E1[:], [[1, 516]], A.is_equal, 0.0, -3, -4), ["E1"], ["EB"])
+    iota(T.JB[:], [[1, C]], -MID, 0, ["JB"])
     fill(T.CS[:, 0:2], 0.0, ["CS0"])
-    fill(T.FL[:, ROW - 1:NV * ROW:ROW], 0.0, ["FLc"])
+    fill(T.FL[:, ROW - 1:K * ROW:ROW], 0.0, ["FLc"])
     fill(T.AC[:, 2 * K - 1:2 * K], float(C - MID), ["a2_%d" % (K - 1)])
     ts(T.PA[:], T.PI[:], 15, None, A.bitwise_and, None, ["PI"], ["PA"])
     cp(T.UO[:], T.UOI[:], ["UOI"], ["UO"])
     cp(T.PM[:], T.PA[:], ["PA"], ["PM"])
     pm, pm1 = T.PM[:, 0:1], T.PM[:, 1:2]
+    ts(T.RP[:, 0:1], pm, 0.0, -float(DROP), A.is_equal, A.mult, ["PM"], ["RP0"])
+    ts(T.CA[:], T.T16[:], pm, float(LIFT), A.is_equal, A.mult, ["T16", "PM"], ["CA"])
+    ts(T.CB[:], T.T16[:], pm1, -float(DROP), A.is_equal, A.mult, ["T16", "PM"], ["CB"])
     ts(T.MASK[:], T.T16[:], pm, None, A.is_equal, None, ["T16", "PM"], ["MASK"])
     ts(T.KEEP[:], T.T16[:], pm, None, A.not_equal, None, ["T16", "PM"], ["KEEP"])
-    ts(T.FL[:, (NV + 1) * ROW - 1:(K - 1) * ROW:ROW], T.KI[:, NV:K - 1], -1.0, float(MID - 16), A.mult, A.add, ["KI"], ["FLs"])
-    ts(T.RP[:, 0:1], pm, 0.0, -float(DROP), A.is_equal, A.mult, ["PM"], ["RP0"])
+    ts(T.QW[:], T.KI[:], pm, None, A.add, None, ["KI", "PM"], ["QW"])
+    tt(T.C0[:], T.CA[:], T.CB[:], A.add, ["CA", "CB"], ["C0"])
+    thr_b, pos_b, off_b, ch_b = T.RP[:, 1:2], T.RP[:, 2:3], T.RP[:, 3:4], T.RP[:, 4:5]
+    base = LIFT - MARK
+    act(thr_b, T.RP[:, 0:1], F_.Identity, ["RP0"], ["RP1"], bias=float(M + C + base))
+    act(pos_b, T.RP[:, 0:1], F_.Identity, ["RP0"], ["RP2"], bias=float(base))
+    act(off_b, T.RP[:, 0:1], F_.Identity, ["RP0"], ["RP3"], bias=float(LIFT - MID))
     quant(T.UQ[:], T.US[:], T.U[:], ["U"], ["UQ", "US"])
+    for a, b in ((KV, KE), (KS, K - 1)):
+        ts(T.FL[:, (a + 1) * ROW - 1:b * ROW:ROW], T.KI[:, a:b], -1.0, float(MID - 16), A.mult, A.add, ["KI"], ["FLc"])
     cp(T.UPQ[:].bitcast(u32), T.UQ[:].bitcast(u32).indirect(T.UO[:]), ["UQ", "UO"], ["UPQ"])
     act(T.UPS[:], T.US[:].indirect(T.UO[:]), F_.Copy, ["US", "UO"], ["UPS"])
-    quant(T.TQ0[:], T.TS0[:], T.X[:], ["X"], ["TQ0"])
-    order("y", ["X"], [])
+    quant_state(0, T.X, [["X0"], ["X1"]])
+    order("y", ["X0", "X1"], [])
     dma("y", T.WQ[:].bitcast(u8), T.wc[:], [], ["WQ"])
     dma("y", T.WS[:], T.ws[:], [], ["WS"])
     dma("y", T.V[:], T.v[:], [], ["V"])
-    thr_b, pos_b, off_b, ch_b = T.RP[:, 1:2], T.RP[:, 2:3], T.RP[:, 3:4], T.RP[:, 4:5]
-    base = LIFT - MARK
 
     for t in range(R):
         dst = T.cores[rank ^ STEP[t]]
         ne = len(topo.engines(dst, core))
         tq, tsc, lq, lsc = T["TQ%d" % t], T["TS%d" % t], T["LQ%d" % t], T["LS%d" % t]
-        rk, lr = T["RK%d" % t], T["LR%d" % t]
-        kq = "TQ%d" % t
+        rk, la, lb = T["RK%d" % t], T["LA%d" % t], T["LB%d" % t]
+        kq = ["TQ%d_0" % t, "TQ%d_1" % t]
         writer["LQ%d" % t] = ("aq%d" % t, 2 * ne, {})
-        writer["LR%d" % t] = ("ar%d" % t, ne, {})
+        writer["LA%d" % t] = ("aa%d" % t, ne, {})
+        writer["LB%d" % t] = ("ab%d" % t, ne, {})
 
-        mm("B0", T.UPQ[:, 0:128], T.UPS[:, 0:128], tq[:], tsc[:], ["UPQ", "UPS", kq])
-        mm("B2", T.UPQ[:, 128:256], T.UPS[:, 128:256], tq[:], tsc[:], ["UPQ", "UPS", kq])
-        mm("B1", T.UPQ[:, 0:128], T.UPS[:, 0:128], tq[:], tsc[:], ["UPQ", "UPS", kq])
-        send(lq[:].bitcast(u8), tq[:].bitcast(u8), "aq%d" % t, dst, [kq])
-        send(lsc[:], tsc[:], "aq%d" % t, dst, [kq])
+        mm("B3", T.UPQ[:, 0:128], T.UPS[:, 0:128], tq[:, 0:MID], tsc[:, 0:MID], ["UPQ", "UPS", kq[0]], MID)
+        mm("B0", T.UPQ[:, 0:128], T.UPS[:, 0:128], tq[:], tsc[:], ["UPQ", "UPS"] + kq)
+        mm("B2", T.UPQ[:, 128:256], T.UPS[:, 128:256], tq[:], tsc[:], ["UPQ", "UPS"] + kq)
+        mm("B1", T.UPQ[:, 0:128], T.UPS[:, 0:128], tq[:], tsc[:], ["UPQ", "UPS"] + kq)
+        send(lq[:].bitcast(u8), tq[:].bitcast(u8), "aq%d" % t, dst, kq)
+        send(lsc[:], tsc[:], "aq%d" % t, dst, kq)
         if t == 0:
-            op("g", lambda: g.affine_select(T.EB[:], T.E1[:], [[1, 516]], A.is_equal, 0.0, -3, -4), ["E1"], ["EB"])
+            ts(T.C2[:, C:C + K], T.QW[:], 2.0, -float(2 * M + L - 1), A.mult, A.add, ["QW"], ["C2w"])
         av, asc = T.B0, T.B1
-        tt(T.MX[:], av[:, 0:C], T.MASK[:], A.mult, ["B0", "MASK"], ["MX"])
+        tt(T.MX[:, 0:MID], T.B3[:, 0:MID], T.MASK[:, 0:MID], A.mult, ["B3", "MASK"], ["MX0"])
+        tt(T.MX[:, MID:C], av[:, MID:C], T.MASK[:, MID:C], A.mult, ["B0", "MASK"], ["MX1"])
         act(T.NS[:], T.B2[:, 0:C], F_.Sign, ["B2"], ["NS"])
-        scan(T.FW[:], T.KEEP[:], T.MX[:], 0.0, A.mult, A.add, ["KEEP", "MX"], ["FW"])
-        act(T.NJ[:], T.NS[:], F_.Relu, ["NS"], ["NJ", "n"], accum_out=T.SM[:, 0:1])
-        tt(T.EQF[:], av[:, 0:C], T.FW[:], A.is_equal, ["B0", "FW"], ["EQF"])
+        for h in range(2):
+            scan(T.FW[:, h * MID:(h + 1) * MID], T.KEEP[:, h * MID:(h + 1) * MID], T.MX[:, h * MID:(h + 1) * MID], 0.0, A.mult, A.add,
+                 ["KEEP", "MX%d" % h], ["FW%d" % h])
 
         def vcount(k):
-            e, o, sc = 16 * k + 16, k * ROW + 1, T.FW[:, 16 * k + 15:16 * k + 16]
-            ts(T.FL[:, o:o + e], av[:, 0:e], sc, 0.5, A.is_lt, A.subtract, ["B0", "FW"], ["fa%d" % k])
-            ts(T.FL[:, o + e:o + C], av[:, e:C], sc, 0.5, A.is_le, A.subtract, ["B0", "FW"], ["fb%d" % k])
+            e, o, sc, fw = 16 * k + 16, k * ROW + 1, T.FW[:, 16 * k + 15:16 * k + 16], "FW%d" % (16 * k // MID)
+            ts(T.FL[:, o:o + e], av[:, 0:e], sc, 0.5, A.is_lt, A.subtract, ["B0", fw], ["fa%d" % k])
+            ts(T.FL[:, o + e:o + C], av[:, e:C], sc, 0.5, A.is_le, A.subtract, ["B0", fw], ["fb%d" % k])
+
+        def vsum(k):
+            j = (k - KE) * HALF
+            scan(T.CL[:, j:j + HALF], T.FL[:, k * ROW:(k + 1) * ROW:2], T.FL[:, k * ROW + 1:(k + 1) * ROW:2], 0.0, A.add, A.add,
+                 ["FL0", "FLc", "fa%d" % k, "fb%d" % k], ["CL%d" % k])
 
         def ssign(k):
             o = k * ROW + 1
-            act(T.FL[:, o:o + C], asc[:, 0:C], F_.Sign, ["B1", "FW"], ["fa%d" % k], bias=T.FW[:, 16 * k + 15:16 * k + 16], scale=-1.0)
+            act(T.FL[:, o:o + C], asc[:, 0:C], F_.Sign, ["B1", "FW%d" % (16 * k // MID)], ["fa%d" % k],
+                bias=T.FW[:, 16 * k + 15:16 * k + 16], scale=-1.0)
 
         def scount(k):
-            e, o, j = 16 * k + 16, k * ROW, (k - NV) * ROW
-            act(T.JK[:, j:j + e + 1], T.FL[:, o:o + e + 1], F_.Relu, ["fa%d" % k, "FL0"], ["ja%d" % k, "a1_%d" % k], accum_out=T.AC[:, k:k + 1])
+            e, o = 16 * k + 16, k * ROW
+            act(T.JK[:, o:o + e + 1], T.FL[:, o:o + e + 1], F_.Relu, ["fa%d" % k, "FL0"], ["ja%d" % k, "a1_%d" % k], accum_out=T.AC[:, k:k + 1])
             if k < K - 1:
-                act(T.JK[:, j + e + 1:j + ROW], T.FL[:, o + e + 1:o + ROW], F_.Relu, ["fa%d" % k, "FLs"], ["jb%d" % k, "a2_%d" % k],
+                act(T.JK[:, o + e + 1:o + ROW], T.FL[:, o + e + 1:o + ROW], F_.Relu, ["fa%d" % k, "FLc"], ["jb%d" % k, "a2_%d" % k],
                     scale=-1.0, accum_out=T.AC[:, K + k:K + k + 1])
 
-        vcount(0)
-        scan(T.COR[:], T.KEEP[:], T.EQF[:], 0.0, A.mult, A.add, ["KEEP", "EQF"], ["COR"])
-        vcount(1)
-        cp(T.FL[:, 0:K * ROW:ROW], T.COR[:, end16], ["COR"], ["FL0"])
-        ssign(NV)
-        act(T.SM[:, 1:2], T.SM[:, 0:1], F_.Relu, ["n"], ["x2"], bias=float(2 * M), scale=-2.0)
-        for k in range(NV, K):
-            if k + 1 < K:
-                ssign(k + 1)
-            scount(k)
-        for k in range(2, NV):
-            vcount(k)
-        scan(T.CS[:, 2:2 + NV * HALF], T.FL[:, 0:NV * ROW:2], T.FL[:, 1:NV * ROW:2], 0.0, A.add, A.add,
-             ["FL0", "FLc"] + ["fa%d" % k for k in range(NV)] + ["fb%d" % k for k in range(NV)], ["CS"])
-        tt(T.WR[:, NV:K], T.AC[:, K + NV:2 * K], T.AC[:, NV:K], A.subtract,
-           ["a1_%d" % k for k in range(NV, K)] + ["a2_%d" % k for k in range(NV, K)], ["WRs"])
-        tt(T.WR[:, 0:NV], T.CS[:, 1:1 + NV * HALF:HALF], T.CS[:, 1 + HALF:2 + NV * HALF:HALF], A.subtract, ["CS", "CS0"], ["WRv"])
-        ts(rk[:], T.WR[:], float(MID), None, A.add, None, ["WRs", "WRv"], ["RK%d" % t])
-        send(lr[:], rk[:], "ar%d" % t, dst, ["RK%d" % t])
+        def sums(a, b):
+            return ["a1_%d" % k for k in range(a, b)] + ["a2_%d" % k for k in range(a, b)]
 
-        if t == 0:
-            ts(T.QW[:], T.KI[:], pm, None, A.add, None, ["KI", "PM"], ["QW"])
-            for b in range(4):
-                quant(T.EQ[:, 128 * b:128 * b + 128], T.ES[:, 128 * b:128 * b + 128], T.EB[:, 3 - b:515 - b], ["EB"], ["EQ%d" % b])
-            ts(T.C2[:, C:C + K], T.QW[:], 2.0, -float(2 * M + L - 1), A.mult, A.add, ["QW"], ["C2w"])
-            ts(T.CA[:], T.T16[:], pm, float(LIFT), A.is_equal, A.mult, ["T16", "PM"], ["CA"])
-            ts(T.CB[:], T.T16[:], pm1, -float(DROP), A.is_equal, A.mult, ["T16", "PM"], ["CB"])
+        vcount(0)
+        tt(T.EQF[:], av[:, 0:C], T.FW[:], A.is_equal, ["B0", "FW0", "FW1"], ["EQF"])
+        vcount(1)
+        scan(T.COR[:], T.KEEP[:], T.EQF[:], 0.0, A.mult, A.add, ["KEEP", "EQF"], ["COR"])
+        vcount(2)
+        cp(T.FL[:, 0:K * ROW:ROW], T.COR[:, end16], ["COR"], ["FL0"])
+        srows = list(range(KV, KE)) + list(range(KS, K))
+        ssign(srows[0])
+        act(T.NJ[:], T.NS[:], F_.Relu, ["NS"], ["NJ", "n"], accum_out=T.SM[:, 0:1])
+        ssign(srows[1])
+        act(T.SM[:, 1:2], T.SM[:, 0:1], F_.Relu, ["n"], ["x2"], bias=float(2 * M), scale=-2.0)
+        ssign(srows[2])
         act(T.AB[:], T.C2[:], F_.Abs, ["C2r", "C2w", "x2"], ["AB"], bias=T.SM[:, 1:2])
-        if t == 0:
-            act(thr_b, T.RP[:, 0:1], F_.Identity, ["RP0"], ["RP1"], bias=float(M + C + base))
-            act(pos_b, T.RP[:, 0:1], F_.Identity, ["RP0"], ["RP2"], bias=float(base))
-            act(off_b, T.RP[:, 0:1], F_.Identity, ["RP0"], ["RP3"], bias=float(LIFT - MID))
-        else:
-            act(T.SM[:, 2:3], T.SM[:, 1:2], F_.Identity, ["x2", "RP1"], ["thr"], bias=thr_b, scale=-0.5)
+        for i, k in enumerate(srows):
+            scount(k)
+            if i + 3 < len(srows):
+                ssign(srows[i + 3])
+        for k in range(3, KV):
+            vcount(k)
+        vcount(KE)
+        scan(T.CS[:, 2:2 + KV * HALF], T.FL[:, 0:KV * ROW:2], T.FL[:, 1:KV * ROW:2], 0.0, A.add, A.add,
+             ["FL0", "FLc"] + ["fa%d" % k for k in range(KV)] + ["fb%d" % k for k in range(KV)], ["CS"])
+        tt(T.WR[:, KV:KE], T.AC[:, K + KV:K + KE], T.AC[:, KV:KE], A.subtract, sums(KV, KE), ["WRs"])
+        vsum(KE)
+        tt(T.WR[:, 0:KV], T.CS[:, 1:1 + KV * HALF:HALF], T.CS[:, 1 + HALF:2 + KV * HALF:HALF], A.subtract, ["CS", "CS0"], ["WRv"])
+        vcount(KE + 1)
+        ts(rk[:, 0:KE], T.WR[:], float(MID), None, A.add, None, ["WRs", "WRv"], ["RKa%d" % t])
+        send(la[:], rk[:, 0:KE], "aa%d" % t, dst, ["RKa%d" % t])
+        for k in range(KE + 2, KS):
+            vcount(k)
+            vsum(k - 1)
+        vsum(KS - 1)
+        tt(T.CL[:, (KS - KE + 1) * HALF - 1:(K - KE) * HALF:HALF], T.AC[:, KS:K], T.AC[:, K + KS:2 * K], A.subtract, sums(KS, K), ["CLs"])
+        ts(rk[:, KE:K], T.CL[:, HALF - 1:(K - KE) * HALF:HALF], -1.0, float(MID), A.mult, A.add,
+           ["CLs"] + ["CL%d" % k for k in range(KE, KS)], ["RKb%d" % t])
+        send(lb[:], rk[:, KE:K], "ab%d" % t, dst, ["RKb%d" % t])
+        krk = ["RKa%d" % t, "RKb%d" % t]
+
         act(T.SG[:], T.AB[:], F_.Sign, ["AB"], ["SG"], bias=-float(L))
-        if t == 0:
-            act(T.SM[:, 2:3], T.SM[:, 1:2], F_.Identity, ["x2", "RP1"], ["thr"], bias=thr_b, scale=-0.5)
+        act(T.SM[:, 2:3], T.SM[:, 1:2], F_.Identity, ["x2", "RP1"], ["thr"], bias=thr_b, scale=-0.5)
         act(T.TAB[:], T.SG[:, 0:C], F_.Copy, ["SG"], ["TAB"], scale=float(MARK))
-        for b in range(4):
-            mm("B%d" % (4 + b), T.EQ[:, 128 * b:128 * b + 128], T.ES[:, 128 * b:128 * b + 128], lq[:], lsc[:], ["EQ%d" % b, "LQ%d" % t])
-        cp(T.H[:, C:2 * C].indirect(rk[:]), T.JB[:], ["JB", "RK%d" % t], ["H"])
-        if t == 0:
-            tt(T.C0[:], T.CA[:], T.CB[:], A.add, ["CA", "CB"], ["C0"])
-        tt(T.ZJ[:], T.TAB[:].indirect(rk[:]), T.JB[:], A.min, ["TAB", "JB", "RK%d" % t], ["ZJ"])
         if t == 0:
             cp(T.CZ[:], T.C0[:], ["C0"], ["CZ"])
+        if t == 1:
+            quant(T.VQ[:], T.VS[:], T.V[:], ["V"], ["VQ"])
+        cp(T.H[:, C:2 * C].indirect(rk[:]), T.JB[:], ["JB"] + krk, ["H"])
+        tt(T.ZJ[:], T.TAB[:].indirect(rk[:]), T.JB[:], A.min, ["TAB", "JB"] + krk, ["ZJ"])
+        if t == 0:
+            tt(T.CZ[:, end16], T.C0[:, end16], T.QW[:], A.add, ["C0", "QW"], ["CZ"])
             act(T.CH[:], T.C0[:], F_.Copy, ["C0"], ["CH"])
             act(ch_b, T.C0[:, 15:16], F_.Identity, ["C0"], ["RP4"], bias=float(C // 2))
-            tt(T.CZ[:, end16], T.C0[:, end16], T.QW[:], A.add, ["C0", "QW"], ["CZ"])
-        act(T.CH[:, end16], T.SG[:, C:C + K], F_.Identity, ["SG", "RP4"], ["CH"], bias=ch_b, scale=float(C // 2))
-        for b in range(4):
-            act(T.WIN[:, (2 * b + 1) * C:(2 * b + 2) * C], T["B%d" % (4 + b)][:, 0:C], F_.Copy, ["B%d" % (4 + b)], ["WD%d" % b], scale=64.0)
-        if t == 0:
             for b in range(4):
-                act(T.WIN[:, 2 * b * C:(2 * b + 1) * C], T.X[:, b:4 * C:4], F_.Copy, ["X"], ["WT%d" % b], scale=64.0)
+                act(T.WIN[:, 2 * b * C:(2 * b + 1) * C], T.X[:, b:4 * C:4], F_.Copy, ["X0", "X1"], ["WT%d" % b], scale=64.0)
 
-        cp(T.ZQ[:].indirect(lr[:]), T.ZJ[:], ["ZJ", "LR%d" % t], ["ZQ"])
+        def unpack(b):
+            mm("B%d" % (4 + b), T.EQ[:, 128 * b:128 * b + 128], T.ES[:, 128 * b:128 * b + 128], lq[:], lsc[:], ["EQ%d" % b, "LQ%d" % t])
+            act(T.WIN[:, (2 * b + 1) * C:(2 * b + 2) * C], T["B%d" % (4 + b)][:, 0:C], F_.Copy, ["B%d" % (4 + b)], ["WD%d" % b], scale=64.0)
+
+        def between(b):
+            if t == 0:
+                quant(T.EQ[:, 128 * b:128 * b + 128], T.ES[:, 128 * b:128 * b + 128], T.EB[:, 3 - b:515 - b], ["EB"], ["EQ%d" % b])
+                unpack(b)
+
+        cp(T.ZQ[:].indirect(la[:]), T.ZJ[:, 0:16 * KE], ["ZJ", "LA%d" % t], ["ZQ"])
+        act(T.CH[:, end16], T.SG[:, C:C + K], F_.Identity, ["SG", "RP4"], ["CH"], bias=ch_b, scale=float(C // 2))
+        if t > 0:
+            for b in range(4):
+                unpack(b)
+        between(0)
+
+        cp(T.ZQ[:].indirect(lb[:]), T.ZJ[:, 16 * KE:C], ["ZJ", "LB%d" % t], ["ZQ"])
+        between(1)
         ts(T.FG[:], T.ZQ[:], -float(MARK // 2), None, A.is_gt, None, ["ZQ"], ["FG"])
         scan(T.VZ[:], T.ZQ[:], T.CZ[:], -4096.0, A.max, A.add, ["ZQ", "CZ"], ["VZ"])
         scan(T.CU[:], T.FG[:], T.MASK[:], float(C - 1 - MARK), A.add, A.min, ["FG", "MASK"], ["CU"])
+        between(2)
         scan(T.VC[:], T.CU[:], T.C0[:], -4096.0, A.max, A.add, ["CU", "C0"], ["VC"])
+        between(3)
         ts(T.T1[:], T.VC[:, end16], T.SM[:, 2:3], float(L), A.is_ge, A.mult, ["VC", "thr"], ["T1"])
         tt(T.T2[:], T.T1[:], T.VC[:, end16], A.add, ["T1", "VC"], ["T2"])
         tt(T.T3[:], T.T2[:], T.VZ[:, end16], A.min, ["T2", "VZ"], ["T3"])
         ts(T.POS[:], T.T3[:], pos_b, None, A.subtract, None, ["T3", "RP2"], ["POS"])
         cp(T.H[:].indirect(T.POS[:]), T.ZQ[:], ["ZQ", "POS"], ["H"])
         scan(T.VH[:], T.H[:, C:2 * C], T.CH[:], -4096.0, A.max, A.add, ["H", "CH"], ["VH"])
-        if t == R - 1:
-            act(T.OT[:], T.H[:, C:2 * C], F_.Identity, ["H"], ["OT"], bias=float(MID))
-            dma("y", T.ot[:], T.OT[0:128:16, :], ["OT"], [])
         ts(T.OFF[:], T.VH[:, end16], off_b, None, A.subtract, None, ["VH", "RP3"], ["OFF"])
 
         for b in range(2):
@@ -313,27 +320,40 @@ def rank_program(g, core, T, topo):
             act(T.F[:, b:4 * C:4], T.WIN[:, 2 * b * C:(2 * b + 2) * C].indirect(T.OFF[:]), F_.Copy,
                 ["WT%d" % b, "WD%d" % b, "OFF"], ["F%d" % b], scale=0.015625)
         quant(T.FQ[:], T.FS[:], T.F[:], ["F%d" % b for b in range(4)], ["FQ"])
-        for b in range(4):
+        for b in range(2):
+            ts(T.F64[:, b * C:(b + 1) * C], T.F[:, b:4 * C:4], 64.0, None, A.mult, None, ["F%d" % b], ["G%d" % b])
+        for b in range(2, 4):
             act(T.F64[:, b * C:(b + 1) * C], T.F[:, b:4 * C:4], F_.Copy, ["F%d" % b], ["G%d" % b], scale=64.0)
         for b in range(4):
             mm("B%d" % b, T.WQ[:, 128 * b:128 * b + 128], T.WS[:, 128 * b:128 * b + 128], T.FQ[:], T.FS[:], ["WQ", "WS", "FQ"])
-        if t == 0:
-            quant(T.VQ[:], T.VS[:], T.V[:], ["V"], ["VQ"])
-        for b in range(4):
+        for b in range(3):
             tt(T.WIN[:, 2 * b * C:(2 * b + 1) * C], T["B%d" % b][:, 0:C], T.F64[:, b * C:(b + 1) * C], A.add, ["B%d" % b, "G%d" % b], ["WT%d" % b])
+        for h in range(2):
+            tt(T.WIN[:, 6 * C + h * MID:6 * C + (h + 1) * MID], T.B3[:, h * MID:(h + 1) * MID], T.F64[:, 3 * C + h * MID:3 * C + (h + 1) * MID],
+               A.add, ["B3", "G3"], ["WT3_%d" % h])
         for b in range(2):
             act(T.TT[:, b:4 * C:4], T.WIN[:, 2 * b * C:(2 * b + 1) * C], F_.Copy, ["WT%d" % b], ["TT%d" % b], scale=0.015625)
-        for b in range(2, 4):
-            ts(T.TT[:, b:4 * C:4], T.WIN[:, 2 * b * C:(2 * b + 1) * C], 0.015625, None, A.mult, None, ["WT%d" % b], ["TT%d" % b])
-        quant(T["TQ%d" % (t + 1)][:], T["TS%d" % (t + 1)][:], T.TT[:], ["TT%d" % b for b in range(4)], ["TQ%d" % (t + 1)])
+        for h in range(2):
+            act(T.TT[:, 2 + 4 * h * MID:4 * (h + 1) * MID:4], T.WIN[:, 4 * C + h * MID:4 * C + (h + 1) * MID], F_.Copy, ["WT2"], ["TT2_%d" % h],
+                scale=0.015625)
+        for h in range(2):
+            ts(T.TT[:, 3 + 4 * h * MID:4 * (h + 1) * MID:4], T.WIN[:, 6 * C + h * MID:6 * C + (h + 1) * MID], 0.015625, None, A.mult, None,
+               ["WT3_%d" % h], ["TT3_%d" % h])
+        writer["WT3"] = writer["WT3_1"]
+        quant_state(t + 1, T.TT, [["TT0", "TT1", "TT2_%d" % h, "TT3_%d" % h] for h in range(2)])
 
-    tq, tsc, kq = T["TQ%d" % R], T["TS%d" % R], "TQ%d" % R
-    mm("B4", T.VQ[:], T.VS[:], tq[:], tsc[:], ["VQ", kq])
-    dma("s", T.oc[:], tq[:].bitcast(u8), [kq], [])
+    tq, tsc, kq = T["TQ%d" % R], T["TS%d" % R], ["TQ%d_0" % R, "TQ%d_1" % R]
+    for h in range(2):
+        mm("B%d" % (4 + h), T.VQ[:], T.VS[:], tq[:, h * MID:(h + 1) * MID], tsc[:, h * MID:(h + 1) * MID], ["VQ", kq[h]], MID)
+    act(T.OT[:], T.H[:, C:2 * C], F_.Identity, ["H"], ["OT"], bias=float(MID))
+    for h in range(2):
+        dma("y", T.oc[:, 4 * h * MID:4 * (h + 1) * MID], tq[:, h * MID:(h + 1) * MID].bitcast(u8), [kq[h]], [])
+    dma("s", T.ot[:], T.OT[0:128:16, :], ["OT"], [])
     for k in range(4):
-        dma("y" if k < 2 else "s", T.osc[4 * k:4 * k + 4, :], tsc[32 * k:32 * k + 4, :], [kq], [])
-    cp(T.Y[:], T.B4[:, 0:C], ["B4"], ["Y"])
-    dma("y", T.y[:], T.Y[:], ["Y"], [])
+        dma("s", T.osc[4 * k:4 * k + 4, :], tsc[32 * k:32 * k + 4, :], kq, [])
+    for h in range(2):
+        cp(T.Y[:, h * MID:(h + 1) * MID], T["B%d" % (4 + h)][:, 0:MID], ["B%d" % (4 + h)], ["Y%d" % h])
+        dma("y", T.y[:, h * MID:(h + 1) * MID], T.Y[:, h * MID:(h + 1) * MID], ["Y%d" % h], [])
     for s, n in count.items():
         if known["g"].get(s, 0) < n:
             g.wait_ge(T.sem[s], n)

@@ -3,30 +3,34 @@ from concourse.mybir import dt, AluOpType, ActivationFunctionType
 C, L, M, R = 320, 96, 224, 3
 STEP = [1, 2, 1]
 K = C // 16
-KV, KE, KS = 9, 12, 16
-ROW = C + 2
-HALF = ROW // 2
+KH = K // 2
+SL = 12
 MID = C // 2
 MARK = 576
 LIFT, DROP = 736, 1792
+SPARE = C + L
+FULL = 16 * (SL - 1)
+BIG = 2.0 ** 96
+TINY = 2.0 ** -120
 BF, F32, F16, Q4, U8, U16, I32 = "bfloat16", "float32", "float16", "float8_e4m3fn_x4", "uint8", "uint16", "int32"
 
 SCRATCH = {}
 for _names, _n, _d in (
         ("X F F64 TT", 4 * C, BF), ("U V", 512, BF), ("UQ VQ", 128, Q4), ("US VS", 128, U8), ("UPQ", 256, Q4), ("UPS", 256, U8),
-        ("WQ EQ", 512, Q4), ("WS ES", 512, U8), ("EB E1", 516, BF), ("FQ TQ0 TQ1 TQ2 TQ3 LQ0 LQ1 LQ2", C, Q4),
-        ("FS TS0 TS1 TS2 TS3 LS0 LS1 LS2", C, U8), ("PI PA", 2, I32), ("PM", 2, F32), ("UOI", 16, I32), ("UO", 16, U16),
-        ("T16 JB MASK KEEP CA CB C0 CH EQF COR NS NJ TAB ZJ ZQ FG", C, BF), ("CZ CU VZ VC VH", C, F16), ("C2 AB", C + K, F32),
-        ("SG", C + K, BF), ("KI QW T1 T2 T3", K, F32), ("RP", 8, F32), ("MX FW OT Y", C, F32), ("FL JK", K * ROW, BF),
-        ("CS", 2 + KV * HALF, F16), ("CL", (K - KE) * HALF, F16), ("AC", 2 * K, F32), ("WR", KE, F32), ("SM", 4, F32),
-        ("POS OFF RK0 RK1 RK2", K, U16), ("LA0 LA1 LA2", KE, U16), ("LB0 LB1 LB2", K - KE, U16), ("H", 2 * C, BF), ("WIN", 8 * C, BF)):
+        ("WQ EQ", 512, Q4), ("WS ES", 512, U8), ("EB", 516, BF), ("FQ TQ0 TQ1 TQ2 TQ3 LQ0 LQ1 LQ2", C, Q4),
+        ("FS TS0 TS1 TS2 TS3 LS0 LS1 LS2", C, U8), ("PI PA", 2, I32), ("PB", 4, I32), ("PM", 2, F32), ("PF", 4, F32), ("UOI", 16, I32),
+        ("UO", 16, U16), ("CA CB CC", 16, BF), ("T16 ROWB D0", MID, BF), ("JB C0 CH DE NS SEG ZJ ZQ FG", C, BF), ("CZ CU VZ VC VH", C, F16),
+        ("C2 AB SG KI QW RT T1 T2 T3", K, F32), ("RP SM", 8, F32), ("MX FW OT Y", C, F32), ("FL", SL * C, BF), ("JS JK", 3 * MID, BF),
+        ("RS", KH * MID, F16), ("RR XX", 32, F32), ("CS0 CS1", 2 + SL * MID // 2, F16), ("D", C + 32, BF),
+        ("Z CK K16 E1", 2 * C + 32, BF), ("LC", 2, U16), ("TAB", 2 * C, BF), ("POS OFF OW RY RK0 RK1 RK2 LK0 LK1 LK2", K, U16),
+        ("H", SPARE + C, BF), ("WIN", 8 * C, BF)):
     for _x in _names.split():
         SCRATCH[_x] = ("sbuf", [128, _n], _d)
 for _t in range(8):
     SCRATCH["B%d" % _t] = ("psum", [128, 512], F32)
 
 SEMAPHORES = (["cv", "cs", "ct", "cg", "sent"] + ["d%d" % i for i in range(16)]
-              + ["%s%d" % (a, t) for a in ("aq", "aa", "ab") for t in range(R)])
+              + ["%s%d" % (a, t) for a in ("aq", "aa") for t in range(R)])
 
 
 def rank_program(g, core, T, topo):
@@ -109,6 +113,9 @@ def rank_program(g, core, T, topo):
     def scan(out, d0, d1, init, op0, op1, reads, writes):
         op("v", lambda: V.tensor_tensor_scan(out, d0, d1, init, op0, op1), reads, writes)
 
+    def turn(out, in_, reads, writes):
+        op("v", lambda: V.transpose(out, in_), reads, writes)
+
     def fill(ap, c, writes):
         op("v", lambda: V.memset(ap, c), [], writes)
 
@@ -117,6 +124,12 @@ def rank_program(g, core, T, topo):
 
     def act(out, in_, f, reads, writes, **kw):
         op("s", lambda: S.activation(out, in_, f, **kw), reads, writes)
+
+    def times(q, out, in_, c, reads, writes):
+        if q == "v":
+            ts(out, in_, c, None, A.mult, None, reads, writes)
+        else:
+            act(out, in_, F_.Copy, reads, writes, scale=c)
 
     def mm(bank, lq, ls, rq, rs, reads, n=C):
         op("t", lambda: P.matmul_mx(T[bank][:, 0:n], lq, ls, rq, rs, True, True), reads, [bank])
@@ -127,233 +140,302 @@ def rank_program(g, core, T, topo):
         else:
             op("g", lambda: g.iota(out, pattern, base, cm), [], writes)
 
-    def quant_state(t, tile, reads):
-        for h in range(2):
-            quant(T["TQ%d" % t][:, h * MID:(h + 1) * MID], T["TS%d" % t][:, h * MID:(h + 1) * MID], tile[:, 4 * h * MID:4 * (h + 1) * MID],
-                  reads[h], ["TQ%d_%d" % (t, h)])
+    def half(buf, h, a=0):
+        return buf[:, a + h * MID:a + (h + 1) * MID]
+
+    def words(buf, h):
+        return buf[:, 4 * h * MID:4 * (h + 1) * MID]
+
+    def plane(buf, b, h):
+        return buf[:, 4 * h * MID + b:4 * (h + 1) * MID:4]
+
+    def flags(slot, a, b):
+        return T.FL[:, SL * a + slot:SL * b:SL]
+
+    def quant_state(t, h, tile, reads):
+        quant(half(T["TQ%d" % t], h), half(T["TS%d" % t], h), words(tile, h), reads, ["TQ%d_%d" % (t, h)])
 
     u8, u32 = dt.uint8, dt.uint32
     end16 = slice(15, C, 16)
 
     dma("y", T.U[:], T.u[:], [], ["U"])
-    dma("y", T.X[:, 0:2 * C], T.x[:, 0:2 * C], [], ["X0"])
-    dma("y", T.X[:, 2 * C:4 * C], T.x[:, 2 * C:4 * C], [], ["X1"])
+    for h in range(2):
+        dma("y", words(T.X, h), words(T.x, h), [], ["X%d" % h])
     iota(T.PI[:], [[15, 2]], 0, 1, ["PI"], False)
+    iota(T.T16[:], [[0, KH], [1, 16]], 0, 0, ["T16"])
     iota(T.UOI[:], [[1, 2], [16, 8]], 0, 0, ["UOI"], False)
-    iota(T.T16[:], [[0, K], [1, 16]], 0, 0, ["T16"])
     iota(T.KI[:], [[16, K]], 0, 0, ["KI"])
-    iota(T.C2[:, 0:C], [[2, C]], -(2 * M + L - 1), 0, ["C2r"])
     fill(T.E1[:], 1.0, ["E1"])
-    op("g", lambda: g.affine_select(T.EB[:], T.E1[:], [[1, 516]], A.is_equal, 0.0, -3, -4), ["E1"], ["EB"])
-    iota(T.JB[:], [[1, C]], -MID, 0, ["JB"])
-    fill(T.CS[:, 0:2], 0.0, ["CS0"])
-    fill(T.FL[:, ROW - 1:K * ROW:ROW], 0.0, ["FLc"])
-    fill(T.AC[:, 2 * K - 1:2 * K], float(C - MID), ["a2_%d" % (K - 1)])
+    op("g", lambda: g.affine_select(T.K16[:], T.E1[:], [[0, 2 * K + 2], [1, 16]], A.not_equal, 0.0, 0, 0), ["E1"], ["K16"])
     ts(T.PA[:], T.PI[:], 15, None, A.bitwise_and, None, ["PI"], ["PA"])
-    cp(T.UO[:], T.UOI[:], ["UOI"], ["UO"])
+    ts(T.PB[:, 0:1], T.PI[:, 0:1], 4, None, A.arith_shift_right, None, ["PI"], ["PB0"])
+    fill(T.CS0[:, 0:1], 0.0, ["CSz0"])
     cp(T.PM[:], T.PA[:], ["PA"], ["PM"])
     pm, pm1 = T.PM[:, 0:1], T.PM[:, 1:2]
-    ts(T.RP[:, 0:1], pm, 0.0, -float(DROP), A.is_equal, A.mult, ["PM"], ["RP0"])
-    ts(T.CA[:], T.T16[:], pm, float(LIFT), A.is_equal, A.mult, ["T16", "PM"], ["CA"])
-    ts(T.CB[:], T.T16[:], pm1, -float(DROP), A.is_equal, A.mult, ["T16", "PM"], ["CB"])
-    ts(T.MASK[:], T.T16[:], pm, None, A.is_equal, None, ["T16", "PM"], ["MASK"])
-    ts(T.KEEP[:], T.T16[:], pm, None, A.not_equal, None, ["T16", "PM"], ["KEEP"])
-    ts(T.QW[:], T.KI[:], pm, None, A.add, None, ["KI", "PM"], ["QW"])
-    tt(T.C0[:], T.CA[:], T.CB[:], A.add, ["CA", "CB"], ["C0"])
-    thr_b, pos_b, off_b, ch_b = T.RP[:, 1:2], T.RP[:, 2:3], T.RP[:, 3:4], T.RP[:, 4:5]
-    base = LIFT - MARK
-    act(thr_b, T.RP[:, 0:1], F_.Identity, ["RP0"], ["RP1"], bias=float(M + C + base))
-    act(pos_b, T.RP[:, 0:1], F_.Identity, ["RP0"], ["RP2"], bias=float(base))
-    act(off_b, T.RP[:, 0:1], F_.Identity, ["RP0"], ["RP3"], bias=float(LIFT - MID))
+    tt(T.PB[:, 1:2], T.PB[:, 0:1], T.PI[:, 0:1], A.add, ["PB0", "PI"], ["PB1"])
+    ts(T.D0[:], T.T16[:], pm, BIG, A.is_equal, A.mult, ["T16", "PM"], ["D0"])
+    ts(T.ROWB[:], T.T16[:], pm, BIG, A.not_equal, A.mult, ["T16", "PM"], ["ROWB"])
+    ts(T.CA[:], T.T16[:, 0:16], pm, float(LIFT), A.is_equal, A.mult, ["T16", "PM"], ["CA"])
+    ts(T.CB[:], T.T16[:, 0:16], pm1, -float(DROP), A.is_equal, A.mult, ["T16", "PM"], ["CB"])
+    ts(T.PB[:, 2:3], T.PB[:, 1:2], 1, None, A.bitwise_and, None, ["PB1"], ["PB2"])
+    cp(T.UO[:], T.UOI[:], ["UOI"], ["UO"])
+    tt(T.CC[:], T.CA[:], T.CB[:], A.add, ["CA", "CB"], ["CC"])
+    ts(T.PF[:, 0:1], T.PB[:, 2:3], float(C + 16), 15.0, A.mult, A.add, ["PB2"], ["PF0"])
+    fill(T.CS1[:, 0:1], 0.0, ["CSz1"])
+    act(half(T.JS, 0), T.T16[:], F_.Sign, ["T16", "PM"], ["JS0"], bias=pm, scale=-1.0)
+    act(T.D0[:, 0:MID:16], T.E1[:, 0:KH], F_.Copy, ["E1"], ["D0"], scale=BIG)
+    act(half(T.JS, 1), half(T.JS, 0), F_.Sign, ["JS0"], ["JS1"], bias=0.5)
+    act(T.QW[:], T.KI[:], F_.Identity, ["KI", "PM"], ["QW"], bias=pm)
+    for h in range(2):
+        act(flags(SL - 1, h * MID, (h + 1) * MID), half(T.JS, 1), F_.Identity, ["JS1"], ["FLc%d" % h], bias=1.5 - h, scale=0.5)
+    zeros = [flags(k, 16 * k, 16 * k + 16) for k in range(KH)] + [T.D[:, 0:16], T.D[:, C + 16:C + 32], T.RR[:, 16:32]]
+    kz = ["z%d" % i for i in range(len(zeros))]
+
+    for z, k in zip(zeros, kz):
+        iota(z, [[0, 16]], 0, 0, [k])
+
+    def pick(i):
+        cp(T.UPQ[:, 128 * i:128 * i + 128].bitcast(u32), T.UQ[:].bitcast(u32).indirect(T.UO[:, 8 * i:8 * i + 8]), ["UQ", "UO"], ["UPQ%d" % i])
+        act(T.UPS[:, 128 * i:128 * i + 128], T.US[:].indirect(T.UO[:, 8 * i:8 * i + 8]), F_.Copy, ["US", "UO"], ["UPS%d" % i])
+
     quant(T.UQ[:], T.US[:], T.U[:], ["U"], ["UQ", "US"])
-    for a, b in ((KV, KE), (KS, K - 1)):
-        ts(T.FL[:, (a + 1) * ROW - 1:b * ROW:ROW], T.KI[:, a:b], -1.0, float(MID - 16), A.mult, A.add, ["KI"], ["FLc"])
-    cp(T.UPQ[:].bitcast(u32), T.UQ[:].bitcast(u32).indirect(T.UO[:]), ["UQ", "UO"], ["UPQ"])
-    act(T.UPS[:], T.US[:].indirect(T.UO[:]), F_.Copy, ["US", "UO"], ["UPS"])
-    quant_state(0, T.X, [["X0"], ["X1"]])
+    ts(T.OW[:], T.KI[:], 0.0, pm, A.mult, A.add, ["KI", "PM"], ["OW"])
+    pick(0)
+    for h in range(2):
+        quant_state(0, h, T.X, ["X%d" % h])
+    pick(1)
     order("y", ["X0", "X1"], [])
     dma("y", T.WQ[:].bitcast(u8), T.wc[:], [], ["WQ"])
     dma("y", T.WS[:], T.ws[:], [], ["WS"])
     dma("y", T.V[:], T.v[:], [], ["V"])
+    thr_b, pos_b, off_b, ch_b = T.RP[:, 1:2], T.RP[:, 2:3], T.RP[:, 3:4], T.RP[:, 4:5]
+    base = LIFT - MARK
+    act(T.PF[:, 2:4], T.QW[:, 0:2], F_.Identity, ["QW", "PF0"], ["PF2"], bias=T.PF[:, 0:1], scale=16.0)
 
     for t in range(R):
         dst = T.cores[rank ^ STEP[t]]
         ne = len(topo.engines(dst, core))
         tq, tsc, lq, lsc = T["TQ%d" % t], T["TS%d" % t], T["LQ%d" % t], T["LS%d" % t]
-        rk, la, lb = T["RK%d" % t], T["LA%d" % t], T["LB%d" % t]
+        rk, lk = T["RK%d" % t], T["LK%d" % t]
         kq = ["TQ%d_0" % t, "TQ%d_1" % t]
         writer["LQ%d" % t] = ("aq%d" % t, 2 * ne, {})
-        writer["LA%d" % t] = ("aa%d" % t, ne, {})
-        writer["LB%d" % t] = ("ab%d" % t, ne, {})
+        writer["LK%d" % t] = ("aa%d" % t, ne, {})
 
-        mm("B3", T.UPQ[:, 0:128], T.UPS[:, 0:128], tq[:, 0:MID], tsc[:, 0:MID], ["UPQ", "UPS", kq[0]], MID)
-        mm("B0", T.UPQ[:, 0:128], T.UPS[:, 0:128], tq[:], tsc[:], ["UPQ", "UPS"] + kq)
-        mm("B2", T.UPQ[:, 128:256], T.UPS[:, 128:256], tq[:], tsc[:], ["UPQ", "UPS"] + kq)
-        mm("B1", T.UPQ[:, 0:128], T.UPS[:, 0:128], tq[:], tsc[:], ["UPQ", "UPS"] + kq)
+        for h in range(2):
+            mm("B%d" % h, T.UPQ[:, 0:128], T.UPS[:, 0:128], half(tq, h), half(tsc, h), ["UPQ0", "UPS0", kq[h]], MID)
+        for i in range(2):
+            mm("B%d" % (2 + i), T.UPQ[:, 128 * i:128 * i + 128], T.UPS[:, 128 * i:128 * i + 128], tq[:], tsc[:], ["UPQ%d" % i, "UPS%d" % i] + kq)
         send(lq[:].bitcast(u8), tq[:].bitcast(u8), "aq%d" % t, dst, kq)
         send(lsc[:], tsc[:], "aq%d" % t, dst, kq)
         if t == 0:
-            ts(T.C2[:, C:C + K], T.QW[:], 2.0, -float(2 * M + L - 1), A.mult, A.add, ["QW"], ["C2w"])
-        av, asc = T.B0, T.B1
-        tt(T.MX[:, 0:MID], T.B3[:, 0:MID], T.MASK[:, 0:MID], A.mult, ["B3", "MASK"], ["MX0"])
-        tt(T.MX[:, MID:C], av[:, MID:C], T.MASK[:, MID:C], A.mult, ["B0", "MASK"], ["MX1"])
-        act(T.NS[:], T.B2[:, 0:C], F_.Sign, ["B2"], ["NS"])
-        for h in range(2):
-            scan(T.FW[:, h * MID:(h + 1) * MID], T.KEEP[:, h * MID:(h + 1) * MID], T.MX[:, h * MID:(h + 1) * MID], 0.0, A.mult, A.add,
-                 ["KEEP", "MX%d" % h], ["FW%d" % h])
+            iota(T.JB[:], [[1, C]], -MID, 0, ["JB"])
+            for a, b, c in ((0, M, MARK), (M, C, -MARK), (C, 2 * C, MARK)):
+                iota(T.TAB[:, a:b], [[0, b - a]], c, 0, ["TAB%d" % a])
+            op("g", lambda: g.affine_select(T.EB[:], T.E1[:, 0:516], [[1, 516]], A.is_equal, 0.0, -3, -4), ["E1"], ["EB"])
+        bank = [T.B0, T.B1]
 
-        def vcount(k):
-            e, o, sc, fw = 16 * k + 16, k * ROW + 1, T.FW[:, 16 * k + 15:16 * k + 16], "FW%d" % (16 * k // MID)
-            ts(T.FL[:, o:o + e], av[:, 0:e], sc, 0.5, A.is_lt, A.subtract, ["B0", fw], ["fa%d" % k])
-            ts(T.FL[:, o + e:o + C], av[:, e:C], sc, 0.5, A.is_le, A.subtract, ["B0", fw], ["fb%d" % k])
+        def mask(h):
+            tt(half(T.MX, h), bank[h][:, 0:MID], T.ROWB[:], A.add, ["B%d" % h, "ROWB"], ["MX%d" % h])
 
-        def vsum(k):
-            j = (k - KE) * HALF
-            scan(T.CL[:, j:j + HALF], T.FL[:, k * ROW:(k + 1) * ROW:2], T.FL[:, k * ROW + 1:(k + 1) * ROW:2], 0.0, A.add, A.add,
-                 ["FL0", "FLc", "fa%d" % k, "fb%d" % k], ["CL%d" % k])
+        def hold(h):
+            scan(half(T.FW, h), T.D0[:], half(T.MX, h), 0.0, A.add, A.min, ["D0", "MX%d" % h], ["FW%d" % h])
+
+        def own(k):
+            return T.FW[:, 16 * k + 15:16 * k + 16]
+
+        def near(h):
+            tt(flags(KH, h * MID, (h + 1) * MID), bank[h][:, 0:MID], half(T.FW, h), A.is_gt, ["B%d" % h, "FW%d" % h], ["n%d" % h])
+
+        def rowkeys(k):
+            return ["r%d_0" % k, "r%d_1" % k]
+
+        def vrow(k, h):
+            if k < KH:
+                a, b, o = [(16 * k + 16, MID, A.is_gt), (MID, MID + 16 * k + 16, A.is_gt)][h]
+            else:
+                a, b, o = [(0, 16 * (k - KH), A.is_ge), (16 * k + 16, C, A.is_gt)][h]
+            if a < b:
+                ts(flags(k % KH, a, b), bank[h][:, a - h * MID:b - h * MID], own(k), None, o, None, ["B%d" % h, "FW%d" % (k // KH)], ["r%d_%d" % (k, h)])
 
         def ssign(k):
-            o = k * ROW + 1
-            act(T.FL[:, o:o + C], asc[:, 0:C], F_.Sign, ["B1", "FW%d" % (16 * k // MID)], ["fa%d" % k],
-                bias=T.FW[:, 16 * k + 15:16 * k + 16], scale=-1.0)
+            act(half(T.JS, k % 3), T.B2[:, 16 * k + 16:16 * k + 16 + MID], F_.Sign, ["B2", "FW0"], ["JS%d" % (k % 3)], bias=own(k), scale=-1.0)
 
-        def scount(k):
-            e, o = 16 * k + 16, k * ROW
-            act(T.JK[:, o:o + e + 1], T.FL[:, o:o + e + 1], F_.Relu, ["fa%d" % k, "FL0"], ["ja%d" % k, "a1_%d" % k], accum_out=T.AC[:, k:k + 1])
-            if k < K - 1:
-                act(T.JK[:, o + e + 1:o + ROW], T.FL[:, o + e + 1:o + ROW], F_.Relu, ["fa%d" % k, "FLc"], ["jb%d" % k, "a2_%d" % k],
-                    scale=-1.0, accum_out=T.AC[:, K + k:K + k + 1])
+        def sflag(k):
+            act(flags(k, 16 * k + 16, 16 * k + 16 + MID), half(T.JS, k % 3), F_.Relu, ["JS%d" % (k % 3)], rowkeys(k) + ["RT%d" % k],
+                scale=-1.0, accum_out=T.RT[:, k:k + 1])
 
-        def sums(a, b):
-            return ["a1_%d" % k for k in range(a, b)] + ["a2_%d" % k for k in range(a, b)]
+        def rowsum(m):
+            scan(half(T.RS, m), T.FL[:, m:SL * C:2 * SL], T.FL[:, m + SL:SL * C:2 * SL], 0.0, A.add, A.add,
+                 [kz[m]] + rowkeys(m) + rowkeys(m + KH), ["RS%d" % m])
 
-        vcount(0)
-        tt(T.EQF[:], av[:, 0:C], T.FW[:], A.is_equal, ["B0", "FW0", "FW1"], ["EQF"])
-        vcount(1)
-        scan(T.COR[:], T.KEEP[:], T.EQF[:], 0.0, A.mult, A.add, ["KEEP", "EQF"], ["COR"])
-        vcount(2)
-        cp(T.FL[:, 0:K * ROW:ROW], T.COR[:, end16], ["COR"], ["FL0"])
-        srows = list(range(KV, KE)) + list(range(KS, K))
-        ssign(srows[0])
-        act(T.NJ[:], T.NS[:], F_.Relu, ["NS"], ["NJ", "n"], accum_out=T.SM[:, 0:1])
-        ssign(srows[1])
-        act(T.SM[:, 1:2], T.SM[:, 0:1], F_.Relu, ["n"], ["x2"], bias=float(2 * M), scale=-2.0)
-        ssign(srows[2])
-        act(T.AB[:], T.C2[:], F_.Abs, ["C2r", "C2w", "x2"], ["AB"], bias=T.SM[:, 1:2])
-        for i, k in enumerate(srows):
-            scount(k)
-            if i + 3 < len(srows):
-                ssign(srows[i + 3])
-        for k in range(3, KV):
-            vcount(k)
-        vcount(KE)
-        scan(T.CS[:, 2:2 + KV * HALF], T.FL[:, 0:KV * ROW:2], T.FL[:, 1:KV * ROW:2], 0.0, A.add, A.add,
-             ["FL0", "FLc"] + ["fa%d" % k for k in range(KV)] + ["fb%d" % k for k in range(KV)], ["CS"])
-        tt(T.WR[:, KV:KE], T.AC[:, K + KV:K + KE], T.AC[:, KV:KE], A.subtract, sums(KV, KE), ["WRs"])
-        vsum(KE)
-        tt(T.WR[:, 0:KV], T.CS[:, 1:1 + KV * HALF:HALF], T.CS[:, 1 + HALF:2 + KV * HALF:HALF], A.subtract, ["CS", "CS0"], ["WRv"])
-        vcount(KE + 1)
-        ts(rk[:, 0:KE], T.WR[:], float(MID), None, A.add, None, ["WRs", "WRv"], ["RKa%d" % t])
-        send(la[:], rk[:, 0:KE], "aa%d" % t, dst, ["RKa%d" % t])
-        for k in range(KE + 2, KS):
-            vcount(k)
-            vsum(k - 1)
-        vsum(KS - 1)
-        tt(T.CL[:, (KS - KE + 1) * HALF - 1:(K - KE) * HALF:HALF], T.AC[:, KS:K], T.AC[:, K + KS:2 * K], A.subtract, sums(KS, K), ["CLs"])
-        ts(rk[:, KE:K], T.CL[:, HALF - 1:(K - KE) * HALF:HALF], -1.0, float(MID), A.mult, A.add,
-           ["CLs"] + ["CL%d" % k for k in range(KE, KS)], ["RKb%d" % t])
-        send(lb[:], rk[:, KE:K], "ab%d" % t, dst, ["RKb%d" % t])
-        krk = ["RKa%d" % t, "RKb%d" % t]
+        def colsum(h):
+            a = SL * MID * h
+            rows = [k for k in range(K - h) if h == 1 or k not in (KH - 1, KH)]
+            scan(T["CS%d" % h][:, 1:1 + SL * MID // 2], T.FL[:, a:a + SL * MID:2], T.FL[:, a + 1:a + SL * MID:2], 0.0, A.add, A.add,
+                 kz + ["FLc%d" % h, "n%d" % h] + ["r%d_%d" % (k, h) for k in rows], ["CS%d" % h])
 
-        act(T.SG[:], T.AB[:], F_.Sign, ["AB"], ["SG"], bias=-float(L))
-        act(T.SM[:, 2:3], T.SM[:, 1:2], F_.Identity, ["x2", "RP1"], ["thr"], bias=thr_b, scale=-0.5)
-        act(T.TAB[:], T.SG[:, 0:C], F_.Copy, ["SG"], ["TAB"], scale=float(MARK))
+        def coldiff(h):
+            cs, n = T["CS%d" % h], SL // 2
+            scan(half(T.D, h, 16), cs[:, n:1 + n * MID:n], cs[:, 0:n * MID:n], 0.0, A.max, A.subtract, ["CS%d" % h, "CSz%d" % h], ["D%d" % h])
+
+        mask(0)
+        hold(0)
+        mask(1)
+        near(0)
+        hold(1)
+        ssign(1)
+        ssign(2)
+        for k in range(1, KH):
+            sflag(k)
+            if k + 2 < KH:
+                ssign(k + 2)
+        for h in range(2):
+            vrow(0, h)
+        near(1)
+        vrow(KH, 1)
+        scan(T.DE[:], T.K16[:, 0:C], flags(KH, 0, C), 0.0, A.mult, A.add, ["K16", "n0", "n1"], ["DE"])
+        for k in range(KH + 1, K):
+            vrow(k, 1)
+            vrow(k, 0)
+        for i, (k, a, b) in enumerate([(0, 16, 16 + MID), (KH, MID + 16, C), (K - 1, 0, MID - 16)]):
+            act(T.JK[:, i * MID:i * MID + b - a], flags(k % KH, a, b), F_.Copy, rowkeys(k), ["JK%d" % i, "RT%d" % k], accum_out=T.RT[:, k:k + 1])
+        m = KH - 1
+        act(T.FG[:], T.B3[:, 0:C], F_.Sign, ["B3"], ["FG", "n"], bias=-TINY, accum_out=T.SM[:, 0:1])
+        if t == 0:
+            act(T.C0[:], T.CC[:].indirect(T.OW[:]), F_.Copy, ["CC", "OW"], ["C0"])
+        act(T.SM[:, 1:2], T.SM[:, 0:1], F_.Relu, ["n"], ["x2"], bias=float(2 * M - C), scale=-1.0)
+        act(T.SM[:, 3:4], T.SM[:, 1:2], F_.Identity, ["x2"], ["zz"], bias=float(FULL), scale=0.5)
+        for k in range(1, m):
+            rowsum(k)
+        for h in range(2):
+            colsum(h)
+        for h in range(2):
+            coldiff(h)
+        if t == 0:
+            ts(T.LC[:], T.PF[:, 2:4], float(2 * C + 31), None, A.min, None, ["PF2"], ["LC"])
+        tt(T.RT[:, KH + 1:KH + m], T.RS[:, 2 * MID - 1:m * MID:MID], T.RT[:, 1:m], A.subtract,
+           ["RS%d" % k for k in range(1, m)] + ["RT%d" % k for k in range(1, m)], ["RTv"])
+        turn(T.Z[:, 0:C], T.D[:, 16:C + 16], ["D0", "D1"], ["ZA"])
+        turn(T.Z[:, C:2 * C + 32], T.D[:], ["D0", "D1"], ["ZB"])
+        tt(T.RR[:, 0:K], T.RT[:], T.DE[:, end16], A.add, ["RTv", "DE"] + ["RT%d" % k for k in range(K)], ["RR"])
+        scan(T.CK[:], T.K16[:], T.Z[:], 0.0, A.mult, A.add, ["K16", "ZA", "ZB"], ["CK"])
         if t == 0:
             cp(T.CZ[:], T.C0[:], ["C0"], ["CZ"])
         if t == 1:
             quant(T.VQ[:], T.VS[:], T.V[:], ["V"], ["VQ"])
-        cp(T.H[:, C:2 * C].indirect(rk[:]), T.JB[:], ["JB"] + krk, ["H"])
-        tt(T.ZJ[:], T.TAB[:].indirect(rk[:]), T.JB[:], A.min, ["TAB", "JB"] + krk, ["ZJ"])
+        tt(T.XX[:], T.CK[:].indirect(T.LC[:]), T.RR[:], A.subtract, ["CK", "LC", "RR"], ["XX"])
         if t == 0:
             tt(T.CZ[:, end16], T.C0[:, end16], T.QW[:], A.add, ["C0", "QW"], ["CZ"])
+        ts(rk[:], T.XX[:, 0:K], -1.0, float(FULL), A.mult, A.add, ["XX"], ["RK%d" % t])
+        send(lk[:], rk[:], "aa%d" % t, dst, ["RK%d" % t])
+        ts(T.RY[:], T.XX[:, 0:K], -1.0, T.SM[:, 3:4], A.mult, A.add, ["XX", "zz"], ["RY"])
+
+        if t == 0:
+            act(T.RP[:, 0:1], pm, F_.Relu, ["PM"], ["RP0"], bias=float(DROP), scale=-float(DROP))
+            act(T.C2[:], T.QW[:], F_.Identity, ["QW"], ["C2"], bias=-float(2 * M + L - 1), scale=2.0)
+            act(thr_b, T.RP[:, 0:1], F_.Identity, ["RP0"], ["RP1"], bias=float(M + SPARE + base), scale=-1.0)
+            act(pos_b, T.RP[:, 0:1], F_.Identity, ["RP0"], ["RP2"], bias=float(base), scale=-1.0)
+            act(off_b, T.RP[:, 0:1], F_.Identity, ["RP0"], ["RP3"], bias=float(LIFT - MID), scale=-1.0)
             act(T.CH[:], T.C0[:], F_.Copy, ["C0"], ["CH"])
             act(ch_b, T.C0[:, 15:16], F_.Identity, ["C0"], ["RP4"], bias=float(C // 2))
-            for b in range(4):
-                act(T.WIN[:, 2 * b * C:(2 * b + 1) * C], T.X[:, b:4 * C:4], F_.Copy, ["X0", "X1"], ["WT%d" % b], scale=64.0)
+        act(T.AB[:], T.C2[:], F_.Abs, ["C2", "x2"], ["AB"], bias=T.SM[:, 1:2])
+        act(T.SM[:, 2:3], T.SM[:, 1:2], F_.Identity, ["x2", "RP1"], ["thr"], bias=thr_b, scale=-0.5)
+        act(T.SG[:], T.AB[:], F_.Sign, ["AB"], ["SG"], bias=-float(L))
 
         def unpack(b):
             mm("B%d" % (4 + b), T.EQ[:, 128 * b:128 * b + 128], T.ES[:, 128 * b:128 * b + 128], lq[:], lsc[:], ["EQ%d" % b, "LQ%d" % t])
-            act(T.WIN[:, (2 * b + 1) * C:(2 * b + 2) * C], T["B%d" % (4 + b)][:, 0:C], F_.Copy, ["B%d" % (4 + b)], ["WD%d" % b], scale=64.0)
+            times("s", T.WIN[:, (2 * b + 1) * C:(2 * b + 2) * C], T["B%d" % (4 + b)][:, 0:C], 64.0, ["B%d" % (4 + b)], ["WD%d" % b])
 
         def between(b):
             if t == 0:
                 quant(T.EQ[:, 128 * b:128 * b + 128], T.ES[:, 128 * b:128 * b + 128], T.EB[:, 3 - b:515 - b], ["EB"], ["EQ%d" % b])
                 unpack(b)
 
-        cp(T.ZQ[:].indirect(la[:]), T.ZJ[:, 0:16 * KE], ["ZJ", "LA%d" % t], ["ZQ"])
-        act(T.CH[:, end16], T.SG[:, C:C + K], F_.Identity, ["SG", "RP4"], ["CH"], bias=ch_b, scale=float(C // 2))
         if t > 0:
-            for b in range(4):
+            for b in range(2):
                 unpack(b)
-        between(0)
+        act(T.SEG[:], T.TAB[:].indirect(T.RY[:]), F_.Copy, ["TAB0", "TAB%d" % M, "TAB%d" % C, "RY"], ["SEG"])
+        act(T.CH[:, end16], T.SG[:], F_.Identity, ["SG", "RP4"], ["CH"], bias=ch_b, scale=float(C // 2))
+        cp(T.H[:, SPARE:SPARE + C].indirect(rk[:]), T.JB[:], ["JB", "RK%d" % t], ["H"])
+        scan(T.ZJ[:], T.JB[:], T.SEG[:], -float(MARK), A.max, A.min, ["JB", "SEG"], ["ZJ"])
+        if t == 0:
+            for b in range(4):
+                times("s", T.WIN[:, 2 * b * C:(2 * b + 1) * C], T.X[:, b:4 * C:4], 64.0, ["X0", "X1"], ["WT%d_0" % b, "WT%d_1" % b])
+        if t > 0:
+            for b in range(2, 4):
+                unpack(b)
 
-        cp(T.ZQ[:].indirect(lb[:]), T.ZJ[:, 16 * KE:C], ["ZJ", "LB%d" % t], ["ZQ"])
-        between(1)
+        cp(T.ZQ[:].indirect(lk[:]), T.ZJ[:], ["ZJ", "LK%d" % t], ["ZQ"])
+        between(0)
         ts(T.FG[:], T.ZQ[:], -float(MARK // 2), None, A.is_gt, None, ["ZQ"], ["FG"])
         scan(T.VZ[:], T.ZQ[:], T.CZ[:], -4096.0, A.max, A.add, ["ZQ", "CZ"], ["VZ"])
-        scan(T.CU[:], T.FG[:], T.MASK[:], float(C - 1 - MARK), A.add, A.min, ["FG", "MASK"], ["CU"])
-        between(2)
+        scan(T.CU[:], T.FG[:], T.TAB[:, C:2 * C], float(SPARE - 1 - MARK), A.add, A.min, ["FG", "TAB%d" % C], ["CU"])
+        between(1)
         scan(T.VC[:], T.CU[:], T.C0[:], -4096.0, A.max, A.add, ["CU", "C0"], ["VC"])
-        between(3)
+        between(2)
         ts(T.T1[:], T.VC[:, end16], T.SM[:, 2:3], float(L), A.is_ge, A.mult, ["VC", "thr"], ["T1"])
-        tt(T.T2[:], T.T1[:], T.VC[:, end16], A.add, ["T1", "VC"], ["T2"])
-        tt(T.T3[:], T.T2[:], T.VZ[:, end16], A.min, ["T2", "VZ"], ["T3"])
+        tt(T.T2[:], T.VC[:, end16], T.VZ[:, end16], A.min, ["VC", "VZ"], ["T2"])
+        between(3)
+        tt(T.T3[:], T.T1[:], T.T2[:], A.add, ["T1", "T2"], ["T3"])
         ts(T.POS[:], T.T3[:], pos_b, None, A.subtract, None, ["T3", "RP2"], ["POS"])
         cp(T.H[:].indirect(T.POS[:]), T.ZQ[:], ["ZQ", "POS"], ["H"])
-        scan(T.VH[:], T.H[:, C:2 * C], T.CH[:], -4096.0, A.max, A.add, ["H", "CH"], ["VH"])
-        ts(T.OFF[:], T.VH[:, end16], off_b, None, A.subtract, None, ["VH", "RP3"], ["OFF"])
+        for h in range(2):
+            scan(half(T.VH, h), half(T.H, h, SPARE), half(T.CH, h), -4096.0, A.max, A.add, ["H", "CH"], ["VH%d" % h])
+        for h in range(2):
+            ts(T.OFF[:, h * KH:(h + 1) * KH], T.VH[:, h * MID + 15:(h + 1) * MID:16], off_b, None, A.subtract, None, ["VH%d" % h, "RP3"], ["OFF%d" % h])
 
-        for b in range(2):
-            ts(T.F[:, b:4 * C:4], T.WIN[:, 2 * b * C:(2 * b + 2) * C].indirect(T.OFF[:]), 0.015625, None, A.mult, None,
-               ["WT%d" % b, "WD%d" % b, "OFF"], ["F%d" % b])
-        for b in range(2, 4):
-            act(T.F[:, b:4 * C:4], T.WIN[:, 2 * b * C:(2 * b + 2) * C].indirect(T.OFF[:]), F_.Copy,
-                ["WT%d" % b, "WD%d" % b, "OFF"], ["F%d" % b], scale=0.015625)
-        quant(T.FQ[:], T.FS[:], T.F[:], ["F%d" % b for b in range(4)], ["FQ"])
-        for b in range(2):
-            ts(T.F64[:, b * C:(b + 1) * C], T.F[:, b:4 * C:4], 64.0, None, A.mult, None, ["F%d" % b], ["G%d" % b])
-        for b in range(2, 4):
-            act(T.F64[:, b * C:(b + 1) * C], T.F[:, b:4 * C:4], F_.Copy, ["F%d" % b], ["G%d" % b], scale=64.0)
-        for b in range(4):
-            mm("B%d" % b, T.WQ[:, 128 * b:128 * b + 128], T.WS[:, 128 * b:128 * b + 128], T.FQ[:], T.FS[:], ["WQ", "WS", "FQ"])
-        for b in range(3):
-            tt(T.WIN[:, 2 * b * C:(2 * b + 1) * C], T["B%d" % b][:, 0:C], T.F64[:, b * C:(b + 1) * C], A.add, ["B%d" % b, "G%d" % b], ["WT%d" % b])
+        def gather(q, b, h):
+            times(q, plane(T.F, b, h), T.WIN[:, 2 * b * C:(2 * b + 2) * C].indirect(T.OFF[:, h * KH:(h + 1) * KH]), 0.015625,
+                  ["WT%d_0" % b, "WT%d_1" % b, "WD%d" % b, "OFF%d" % h], ["F%d_%d" % (b, h)])
+
+        def layer(h):
+            quant(half(T.FQ, h), half(T.FS, h), words(T.F, h), ["F%d_%d" % (b, h) for b in range(4)], ["FQ%d" % h])
+            for b in range(4):
+                mm("B%d" % (4 * h + b), T.WQ[:, 128 * b:128 * b + 128], T.WS[:, 128 * b:128 * b + 128], half(T.FQ, h), half(T.FS, h),
+                   ["WQ", "WS", "FQ%d" % h], MID)
+
+        def widen(q, h):
+            times(q, words(T.F64, h), words(T.F, h), 64.0, ["F%d_%d" % (b, h) for b in range(4)], ["G%d" % h])
+
+        def add(b, h):
+            tt(half(T.WIN, h, 2 * b * C), T["B%d" % (4 * h + b)][:, 0:MID], plane(T.F64, b, h), A.add, ["B%d" % (4 * h + b), "G%d" % h], ["WT%d_%d" % (b, h)])
+
+        def scale(q, b, h):
+            times(q, plane(T.TT, b, h), half(T.WIN, h, 2 * b * C), 0.015625, ["WT%d_%d" % (b, h)], ["TT%d_%d" % (b, h)])
+
+        def state(h):
+            quant_state(t + 1, h, T.TT, ["TT%d_%d" % (b, h) for b in range(4)])
+
+        for q, b, h in (("v", 0, 0), ("v", 1, 0), ("s", 2, 0), ("s", 3, 0), ("s", 2, 1), ("s", 3, 1), ("s", 1, 1)):
+            gather(q, b, h)
+        layer(0)
+        gather("v", 0, 1)
+        widen("v", 0)
+        layer(1)
+        widen("s", 1)
         for h in range(2):
-            tt(T.WIN[:, 6 * C + h * MID:6 * C + (h + 1) * MID], T.B3[:, h * MID:(h + 1) * MID], T.F64[:, 3 * C + h * MID:3 * C + (h + 1) * MID],
-               A.add, ["B3", "G3"], ["WT3_%d" % h])
-        for b in range(2):
-            act(T.TT[:, b:4 * C:4], T.WIN[:, 2 * b * C:(2 * b + 1) * C], F_.Copy, ["WT%d" % b], ["TT%d" % b], scale=0.015625)
-        for h in range(2):
-            act(T.TT[:, 2 + 4 * h * MID:4 * (h + 1) * MID:4], T.WIN[:, 4 * C + h * MID:4 * C + (h + 1) * MID], F_.Copy, ["WT2"], ["TT2_%d" % h],
-                scale=0.015625)
-        for h in range(2):
-            ts(T.TT[:, 3 + 4 * h * MID:4 * (h + 1) * MID:4], T.WIN[:, 6 * C + h * MID:6 * C + (h + 1) * MID], 0.015625, None, A.mult, None,
-               ["WT3_%d" % h], ["TT3_%d" % h])
-        writer["WT3"] = writer["WT3_1"]
-        quant_state(t + 1, T.TT, [["TT0", "TT1", "TT2_%d" % h, "TT3_%d" % h] for h in range(2)])
+            for b in range(4):
+                add(b, h)
+                if b < 3:
+                    scale("s", b, h)
+                if (b, h) == (0, 1):
+                    scale("v", 3, 0)
+        state(0)
+        scale("v", 3, 1)
+        state(1)
 
     tq, tsc, kq = T["TQ%d" % R], T["TS%d" % R], ["TQ%d_0" % R, "TQ%d_1" % R]
+    act(T.OT[:], T.H[:, SPARE:SPARE + C], F_.Identity, ["H"], ["OT"], bias=float(MID))
     for h in range(2):
-        mm("B%d" % (4 + h), T.VQ[:], T.VS[:], tq[:, h * MID:(h + 1) * MID], tsc[:, h * MID:(h + 1) * MID], ["VQ", kq[h]], MID)
-    act(T.OT[:], T.H[:, C:2 * C], F_.Identity, ["H"], ["OT"], bias=float(MID))
+        mm("B%d" % h, T.VQ[:], T.VS[:], half(tq, h), half(tsc, h), ["VQ", kq[h]], MID)
     for h in range(2):
-        dma("y", T.oc[:, 4 * h * MID:4 * (h + 1) * MID], tq[:, h * MID:(h + 1) * MID].bitcast(u8), [kq[h]], [])
+        dma("y", words(T.oc, h), half(tq, h).bitcast(u8), [kq[h]], [])
     dma("s", T.ot[:], T.OT[0:128:16, :], ["OT"], [])
     for k in range(4):
         dma("s", T.osc[4 * k:4 * k + 4, :], tsc[32 * k:32 * k + 4, :], kq, [])
     for h in range(2):
-        cp(T.Y[:, h * MID:(h + 1) * MID], T["B%d" % (4 + h)][:, 0:MID], ["B%d" % (4 + h)], ["Y%d" % h])
-        dma("y", T.y[:, h * MID:(h + 1) * MID], T.Y[:, h * MID:(h + 1) * MID], ["Y%d" % h], [])
+        cp(half(T.Y, h), T["B%d" % h][:, 0:MID], ["B%d" % h], ["Y%d" % h])
+        dma("y", half(T.y, h), half(T.Y, h), ["Y%d" % h], [])
     for s, n in count.items():
         if known["g"].get(s, 0) < n:
             g.wait_ge(T.sem[s], n)

from concourse.mybir import dt, AluOpType, ActivationFunctionType

C, L, M, R = 320, 96, 224, 3
STEP = [1, 2, 1]
K = C // 16
KH = K // 2
SL = 12
MID = C // 2
MARK = 576
LIFT, DROP = 736, 1792
SPARE = C + L
FULL = 16 * (SL - 1)
BIG = 2.0 ** 96
TINY = 2.0 ** -120
BF, F32, F16, Q4, U8, U16, I32 = "bfloat16", "float32", "float16", "float8_e4m3fn_x4", "uint8", "uint16", "int32"

SCRATCH = {}
for _names, _n, _d in (
        ("X F F64 TT", 4 * C, BF), ("U V", 512, BF), ("UQ VQ", 128, Q4), ("US VS", 128, U8), ("UPQ", 256, Q4), ("UPS", 256, U8),
        ("WQ EQ", 512, Q4), ("WS ES", 512, U8), ("EB", 516, BF), ("FQ TQ0 TQ1 TQ2 TQ3 LQ0 LQ1 LQ2", C, Q4),
        ("FS TS0 TS1 TS2 TS3 LS0 LS1 LS2", C, U8), ("PI PA", 2, I32), ("PB", 4, I32), ("PM", 2, F32), ("PF", 4, F32), ("UOI", 16, I32),
        ("UO", 16, U16), ("CA CB CC", 16, BF), ("T16 ROWB D0", MID, BF), ("JB C0 CH DE NS SEG ZJ ZQ FG", C, BF), ("CZ CU VZ VC VH", C, F16),
        ("C2 AB SG KI QW RT T1 T2 T3", K, F32), ("RP SM", 8, F32), ("MX FW OT Y", C, F32), ("FL", SL * C, BF), ("JS JK", 3 * MID, BF),
        ("RS", KH * MID, F16), ("RR XX", 32, F32), ("CS0 CS1", 2 + SL * MID // 2, F16), ("D", C + 32, BF),
        ("Z CK K16 E1", 2 * C + 32, BF), ("LC", 2, U16), ("TAB", 2 * C, BF), ("POS OFF OW RY RK0 RK1 RK2 LK0 LK1 LK2", K, U16),
        ("H", SPARE + C, BF), ("WIN", 8 * C, BF)):
    for _x in _names.split():
        SCRATCH[_x] = ("sbuf", [128, _n], _d)
for _t in range(8):
    SCRATCH["B%d" % _t] = ("psum", [128, 512], F32)

SEMAPHORES = (["cv", "cs", "ct", "cg", "sent"] + ["d%d" % i for i in range(16)]
              + ["%s%d" % (a, t) for a in ("aq", "aa") for t in range(R)])


def rank_program(g, core, T, topo):
    rank = T.rank_of(core)
    if rank is None:
        return
    A, F_ = AluOpType, ActivationFunctionType
    queue = {"v": g.vector, "s": g.scalar, "t": g.tensor, "g": g, "y": g.sync}
    count = {"cv": 0, "cs": 0, "ct": 0, "cg": 0, "sent": 0}
    known = {q: {} for q in queue}
    writer, readers = {}, {}
    ndma = [0]

    def settle(q, events):
        need = {}
        for s, n, kn in events:
            if known[q].get(s, 0) < n and need.get(s, (0, None))[0] < n:
                need[s] = (n, kn)
        for s in list(need):
            n = need[s][0]
            if any(o != s and need[o][1].get(s, 0) >= n for o in need):
                del need[s]
        for s, (n, kn) in need.items():
            queue[q].wait_ge(T.sem[s], n)
            known[q][s] = n
            for a, b in kn.items():
                if known[q].get(a, 0) < b:
                    known[q][a] = b

    def order(q, reads, writes):
        ev = [writer[k] for k in reads if k in writer]
        for k in writes:
            if k in writer:
                ev.append(writer[k])
            ev.extend(readers.get(k, []))
        settle(q, ev)

    def note(e, reads, writes):
        for k in reads:
            readers.setdefault(k, []).append(e)
        for k in writes:
            writer[k] = e
            readers[k] = []

    def op(q, call, reads, writes):
        order(q, reads, writes)
        s = "c" + q
        call().then_inc(T.sem[s], 1)
        count[s] += 1
        note((s, count[s], dict(known[q])), reads, writes)

    def dma(q, out, in_, reads, writes):
        order(q, reads, writes)
        s = "d%d" % ndma[0]
        ndma[0] += 1
        queue[q].dma_start(out, in_).then_inc(T.sem[s], 16)
        count[s] = 16
        note((s, 16, dict(known[q])), reads, writes)

    def send(out, in_, sem, dst, reads):
        order("g", reads, [])
        rid, pid, _ = topo.addr(dst)
        g.remote_dma(out, in_, T.sem[sem], T.sem.sent, pid, rid, topo.mask(core, dst))
        count["sent"] += len(topo.engines(core, dst))

    V, S, P = g.vector, g.scalar, g.tensor

    def ts(out, in0, s1, s2, op0, op1, reads, writes):
        if op1 is None:
            op("v", lambda: V.tensor_scalar(out, in0, s1, None, op0), reads, writes)
        else:
            op("v", lambda: V.tensor_scalar(out, in0, s1, s2, op0, op1), reads, writes)

    def tt(out, in0, in1, o, reads, writes):
        op("v", lambda: V.tensor_tensor(out, in0, in1, o), reads, writes)

    def cp(out, in_, reads, writes):
        op("v", lambda: V.tensor_copy(out, in_), reads, writes)

    def scan(out, d0, d1, init, op0, op1, reads, writes):
        op("v", lambda: V.tensor_tensor_scan(out, d0, d1, init, op0, op1), reads, writes)

    def turn(out, in_, reads, writes):
        op("v", lambda: V.transpose(out, in_), reads, writes)

    def fill(ap, c, writes):
        op("v", lambda: V.memset(ap, c), [], writes)

    def quant(q, s, in_, reads, writes):
        op("v", lambda: V.quantize_mx(q, s, in_), reads, writes)

    def act(out, in_, f, reads, writes, **kw):
        op("s", lambda: S.activation(out, in_, f, **kw), reads, writes)

    def times(q, out, in_, c, reads, writes):
        if q == "v":
            ts(out, in_, c, None, A.mult, None, reads, writes)
        else:
            act(out, in_, F_.Copy, reads, writes, scale=c)

    def mm(bank, lq, ls, rq, rs, reads, n=C):
        op("t", lambda: P.matmul_mx(T[bank][:, 0:n], lq, ls, rq, rs, True, True), reads, [bank])

    def iota(out, pattern, base, cm, writes, small=True):
        if small:
            op("g", lambda: g.iota(out, pattern, base, cm, allow_small_or_imprecise_dtypes=True), [], writes)
        else:
            op("g", lambda: g.iota(out, pattern, base, cm), [], writes)

    def half(buf, h, a=0):
        return buf[:, a + h * MID:a + (h + 1) * MID]

    def words(buf, h):
        return buf[:, 4 * h * MID:4 * (h + 1) * MID]

    def plane(buf, b, h):
        return buf[:, 4 * h * MID + b:4 * (h + 1) * MID:4]

    def flags(slot, a, b):
        return T.FL[:, SL * a + slot:SL * b:SL]

    def quant_state(t, h, tile, reads):
        quant(half(T["TQ%d" % t], h), half(T["TS%d" % t], h), words(tile, h), reads, ["TQ%d_%d" % (t, h)])

    u8, u32 = dt.uint8, dt.uint32
    end16 = slice(15, C, 16)

    dma("y", T.U[:], T.u[:], [], ["U"])
    for h in range(2):
        dma("y", words(T.X, h), words(T.x, h), [], ["X%d" % h])
    iota(T.PI[:], [[15, 2]], 0, 1, ["PI"], False)
    iota(T.T16[:], [[0, KH], [1, 16]], 0, 0, ["T16"])
    iota(T.UOI[:], [[1, 2], [16, 8]], 0, 0, ["UOI"], False)
    iota(T.KI[:], [[16, K]], 0, 0, ["KI"])
    fill(T.E1[:], 1.0, ["E1"])
    op("g", lambda: g.affine_select(T.K16[:], T.E1[:], [[0, 2 * K + 2], [1, 16]], A.not_equal, 0.0, 0, 0), ["E1"], ["K16"])
    ts(T.PA[:], T.PI[:], 15, None, A.bitwise_and, None, ["PI"], ["PA"])
    ts(T.PB[:, 0:1], T.PI[:, 0:1], 4, None, A.arith_shift_right, None, ["PI"], ["PB0"])
    fill(T.CS0[:, 0:1], 0.0, ["CSz0"])
    cp(T.PM[:], T.PA[:], ["PA"], ["PM"])
    pm, pm1 = T.PM[:, 0:1], T.PM[:, 1:2]
    tt(T.PB[:, 1:2], T.PB[:, 0:1], T.PI[:, 0:1], A.add, ["PB0", "PI"], ["PB1"])
    ts(T.D0[:], T.T16[:], pm, BIG, A.is_equal, A.mult, ["T16", "PM"], ["D0"])
    ts(T.ROWB[:], T.T16[:], pm, BIG, A.not_equal, A.mult, ["T16", "PM"], ["ROWB"])
    ts(T.CA[:], T.T16[:, 0:16], pm, float(LIFT), A.is_equal, A.mult, ["T16", "PM"], ["CA"])
    ts(T.CB[:], T.T16[:, 0:16], pm1, -float(DROP), A.is_equal, A.mult, ["T16", "PM"], ["CB"])
    ts(T.PB[:, 2:3], T.PB[:, 1:2], 1, None, A.bitwise_and, None, ["PB1"], ["PB2"])
    cp(T.UO[:], T.UOI[:], ["UOI"], ["UO"])
    tt(T.CC[:], T.CA[:], T.CB[:], A.add, ["CA", "CB"], ["CC"])
    ts(T.PF[:, 0:1], T.PB[:, 2:3], float(C + 16), 15.0, A.mult, A.add, ["PB2"], ["PF0"])
    fill(T.CS1[:, 0:1], 0.0, ["CSz1"])
    act(half(T.JS, 0), T.T16[:], F_.Sign, ["T16", "PM"], ["JS0"], bias=pm, scale=-1.0)
    act(T.D0[:, 0:MID:16], T.E1[:, 0:KH], F_.Copy, ["E1"], ["D0"], scale=BIG)
    act(half(T.JS, 1), half(T.JS, 0), F_.Sign, ["JS0"], ["JS1"], bias=0.5)
    act(T.QW[:], T.KI[:], F_.Identity, ["KI", "PM"], ["QW"], bias=pm)
    for h in range(2):
        act(flags(SL - 1, h * MID, (h + 1) * MID), half(T.JS, 1), F_.Identity, ["JS1"], ["FLc%d" % h], bias=1.5 - h, scale=0.5)
    zeros = [flags(k, 16 * k, 16 * k + 16) for k in range(KH)] + [T.D[:, 0:16], T.D[:, C + 16:C + 32], T.RR[:, 16:32]]
    kz = ["z%d" % i for i in range(len(zeros))]

    for z, k in zip(zeros, kz):
        iota(z, [[0, 16]], 0, 0, [k])

    def pick(i):
        cp(T.UPQ[:, 128 * i:128 * i + 128].bitcast(u32), T.UQ[:].bitcast(u32).indirect(T.UO[:, 8 * i:8 * i + 8]), ["UQ", "UO"], ["UPQ%d" % i])
        act(T.UPS[:, 128 * i:128 * i + 128], T.US[:].indirect(T.UO[:, 8 * i:8 * i + 8]), F_.Copy, ["US", "UO"], ["UPS%d" % i])

    quant(T.UQ[:], T.US[:], T.U[:], ["U"], ["UQ", "US"])
    ts(T.OW[:], T.KI[:], 0.0, pm, A.mult, A.add, ["KI", "PM"], ["OW"])
    pick(0)
    for h in range(2):
        quant_state(0, h, T.X, ["X%d" % h])
    pick(1)
    order("y", ["X0", "X1"], [])
    dma("y", T.WQ[:].bitcast(u8), T.wc[:], [], ["WQ"])
    dma("y", T.WS[:], T.ws[:], [], ["WS"])
    dma("y", T.V[:], T.v[:], [], ["V"])
    thr_b, pos_b, off_b, ch_b = T.RP[:, 1:2], T.RP[:, 2:3], T.RP[:, 3:4], T.RP[:, 4:5]
    base = LIFT - MARK
    act(T.PF[:, 2:4], T.QW[:, 0:2], F_.Identity, ["QW", "PF0"], ["PF2"], bias=T.PF[:, 0:1], scale=16.0)

    for t in range(R):
        dst = T.cores[rank ^ STEP[t]]
        ne = len(topo.engines(dst, core))
        tq, tsc, lq, lsc = T["TQ%d" % t], T["TS%d" % t], T["LQ%d" % t], T["LS%d" % t]
        rk, lk = T["RK%d" % t], T["LK%d" % t]
        kq = ["TQ%d_0" % t, "TQ%d_1" % t]
        writer["LQ%d" % t] = ("aq%d" % t, 2 * ne, {})
        writer["LK%d" % t] = ("aa%d" % t, ne, {})

        for h in range(2):
            mm("B%d" % h, T.UPQ[:, 0:128], T.UPS[:, 0:128], half(tq, h), half(tsc, h), ["UPQ0", "UPS0", kq[h]], MID)
        for i in range(2):
            mm("B%d" % (2 + i), T.UPQ[:, 128 * i:128 * i + 128], T.UPS[:, 128 * i:128 * i + 128], tq[:], tsc[:], ["UPQ%d" % i, "UPS%d" % i] + kq)
        send(lq[:].bitcast(u8), tq[:].bitcast(u8), "aq%d" % t, dst, kq)
        send(lsc[:], tsc[:], "aq%d" % t, dst, kq)
        if t == 0:
            iota(T.JB[:], [[1, C]], -MID, 0, ["JB"])
            for a, b, c in ((0, M, MARK), (M, C, -MARK), (C, 2 * C, MARK)):
                iota(T.TAB[:, a:b], [[0, b - a]], c, 0, ["TAB%d" % a])
            op("g", lambda: g.affine_select(T.EB[:], T.E1[:, 0:516], [[1, 516]], A.is_equal, 0.0, -3, -4), ["E1"], ["EB"])
        bank = [T.B0, T.B1]

        def mask(h):
            tt(half(T.MX, h), bank[h][:, 0:MID], T.ROWB[:], A.add, ["B%d" % h, "ROWB"], ["MX%d" % h])

        def hold(h):
            scan(half(T.FW, h), T.D0[:], half(T.MX, h), 0.0, A.add, A.min, ["D0", "MX%d" % h], ["FW%d" % h])

        def own(k):
            return T.FW[:, 16 * k + 15:16 * k + 16]

        def near(h):
            tt(flags(KH, h * MID, (h + 1) * MID), bank[h][:, 0:MID], half(T.FW, h), A.is_gt, ["B%d" % h, "FW%d" % h], ["n%d" % h])

        def rowkeys(k):
            return ["r%d_0" % k, "r%d_1" % k]

        def vrow(k, h):
            if k < KH:
                a, b, o = [(16 * k + 16, MID, A.is_gt), (MID, MID + 16 * k + 16, A.is_gt)][h]
            else:
                a, b, o = [(0, 16 * (k - KH), A.is_ge), (16 * k + 16, C, A.is_gt)][h]
            if a < b:
                ts(flags(k % KH, a, b), bank[h][:, a - h * MID:b - h * MID], own(k), None, o, None, ["B%d" % h, "FW%d" % (k // KH)], ["r%d_%d" % (k, h)])

        def ssign(k):
            act(half(T.JS, k % 3), T.B2[:, 16 * k + 16:16 * k + 16 + MID], F_.Sign, ["B2", "FW0"], ["JS%d" % (k % 3)], bias=own(k), scale=-1.0)

        def sflag(k):
            act(flags(k, 16 * k + 16, 16 * k + 16 + MID), half(T.JS, k % 3), F_.Relu, ["JS%d" % (k % 3)], rowkeys(k) + ["RT%d" % k],
                scale=-1.0, accum_out=T.RT[:, k:k + 1])

        def rowsum(m):
            scan(half(T.RS, m), T.FL[:, m:SL * C:2 * SL], T.FL[:, m + SL:SL * C:2 * SL], 0.0, A.add, A.add,
                 [kz[m]] + rowkeys(m) + rowkeys(m + KH), ["RS%d" % m])

        def colsum(h):
            a = SL * MID * h
            rows = [k for k in range(K - h) if h == 1 or k not in (KH - 1, KH)]
            scan(T["CS%d" % h][:, 1:1 + SL * MID // 2], T.FL[:, a:a + SL * MID:2], T.FL[:, a + 1:a + SL * MID:2], 0.0, A.add, A.add,
                 kz + ["FLc%d" % h, "n%d" % h] + ["r%d_%d" % (k, h) for k in rows], ["CS%d" % h])

        def coldiff(h):
            cs, n = T["CS%d" % h], SL // 2
            scan(half(T.D, h, 16), cs[:, n:1 + n * MID:n], cs[:, 0:n * MID:n], 0.0, A.max, A.subtract, ["CS%d" % h, "CSz%d" % h], ["D%d" % h])

        mask(0)
        hold(0)
        mask(1)
        near(0)
        hold(1)
        ssign(1)
        ssign(2)
        for k in range(1, KH):
            sflag(k)
            if k + 2 < KH:
                ssign(k + 2)
        for h in range(2):
            vrow(0, h)
        near(1)
        vrow(KH, 1)
        scan(T.DE[:], T.K16[:, 0:C], flags(KH, 0, C), 0.0, A.mult, A.add, ["K16", "n0", "n1"], ["DE"])
        for k in range(KH + 1, K):
            vrow(k, 1)
            vrow(k, 0)
        for i, (k, a, b) in enumerate([(0, 16, 16 + MID), (KH, MID + 16, C), (K - 1, 0, MID - 16)]):
            act(T.JK[:, i * MID:i * MID + b - a], flags(k % KH, a, b), F_.Copy, rowkeys(k), ["JK%d" % i, "RT%d" % k], accum_out=T.RT[:, k:k + 1])
        m = KH - 1
        act(T.FG[:], T.B3[:, 0:C], F_.Sign, ["B3"], ["FG", "n"], bias=-TINY, accum_out=T.SM[:, 0:1])
        if t == 0:
            act(T.C0[:], T.CC[:].indirect(T.OW[:]), F_.Copy, ["CC", "OW"], ["C0"])
        act(T.SM[:, 1:2], T.SM[:, 0:1], F_.Relu, ["n"], ["x2"], bias=float(2 * M - C), scale=-1.0)
        act(T.SM[:, 3:4], T.SM[:, 1:2], F_.Identity, ["x2"], ["zz"], bias=float(FULL), scale=0.5)
        for k in range(1, m):
            rowsum(k)
        for h in range(2):
            colsum(h)
        for h in range(2):
            coldiff(h)
        if t == 0:
            ts(T.LC[:], T.PF[:, 2:4], float(2 * C + 31), None, A.min, None, ["PF2"], ["LC"])
        tt(T.RT[:, KH + 1:KH + m], T.RS[:, 2 * MID - 1:m * MID:MID], T.RT[:, 1:m], A.subtract,
           ["RS%d" % k for k in range(1, m)] + ["RT%d" % k for k in range(1, m)], ["RTv"])
        turn(T.Z[:, 0:C], T.D[:, 16:C + 16], ["D0", "D1"], ["ZA"])
        turn(T.Z[:, C:2 * C + 32], T.D[:], ["D0", "D1"], ["ZB"])
        tt(T.RR[:, 0:K], T.RT[:], T.DE[:, end16], A.add, ["RTv", "DE"] + ["RT%d" % k for k in range(K)], ["RR"])
        scan(T.CK[:], T.K16[:], T.Z[:], 0.0, A.mult, A.add, ["K16", "ZA", "ZB"], ["CK"])
        if t == 0:
            cp(T.CZ[:], T.C0[:], ["C0"], ["CZ"])
        if t == 1:
            quant(T.VQ[:], T.VS[:], T.V[:], ["V"], ["VQ"])
        tt(T.XX[:], T.CK[:].indirect(T.LC[:]), T.RR[:], A.subtract, ["CK", "LC", "RR"], ["XX"])
        if t == 0:
            tt(T.CZ[:, end16], T.C0[:, end16], T.QW[:], A.add, ["C0", "QW"], ["CZ"])
        ts(rk[:], T.XX[:, 0:K], -1.0, float(FULL), A.mult, A.add, ["XX"], ["RK%d" % t])
        send(lk[:], rk[:], "aa%d" % t, dst, ["RK%d" % t])
        ts(T.RY[:], T.XX[:, 0:K], -1.0, T.SM[:, 3:4], A.mult, A.add, ["XX", "zz"], ["RY"])

        if t == 0:
            act(T.RP[:, 0:1], pm, F_.Relu, ["PM"], ["RP0"], bias=float(DROP), scale=-float(DROP))
            act(T.C2[:], T.QW[:], F_.Identity, ["QW"], ["C2"], bias=-float(2 * M + L - 1), scale=2.0)
            act(thr_b, T.RP[:, 0:1], F_.Identity, ["RP0"], ["RP1"], bias=float(M + SPARE + base), scale=-1.0)
            act(pos_b, T.RP[:, 0:1], F_.Identity, ["RP0"], ["RP2"], bias=float(base), scale=-1.0)
            act(off_b, T.RP[:, 0:1], F_.Identity, ["RP0"], ["RP3"], bias=float(LIFT - MID), scale=-1.0)
            act(T.CH[:], T.C0[:], F_.Copy, ["C0"], ["CH"])
            act(ch_b, T.C0[:, 15:16], F_.Identity, ["C0"], ["RP4"], bias=float(C // 2))
        act(T.AB[:], T.C2[:], F_.Abs, ["C2", "x2"], ["AB"], bias=T.SM[:, 1:2])
        act(T.SM[:, 2:3], T.SM[:, 1:2], F_.Identity, ["x2", "RP1"], ["thr"], bias=thr_b, scale=-0.5)
        act(T.SG[:], T.AB[:], F_.Sign, ["AB"], ["SG"], bias=-float(L))

        def unpack(b):
            mm("B%d" % (4 + b), T.EQ[:, 128 * b:128 * b + 128], T.ES[:, 128 * b:128 * b + 128], lq[:], lsc[:], ["EQ%d" % b, "LQ%d" % t])
            times("s", T.WIN[:, (2 * b + 1) * C:(2 * b + 2) * C], T["B%d" % (4 + b)][:, 0:C], 64.0, ["B%d" % (4 + b)], ["WD%d" % b])

        def between(b):
            if t == 0:
                quant(T.EQ[:, 128 * b:128 * b + 128], T.ES[:, 128 * b:128 * b + 128], T.EB[:, 3 - b:515 - b], ["EB"], ["EQ%d" % b])
                unpack(b)

        if t > 0:
            for b in range(2):
                unpack(b)
        act(T.SEG[:], T.TAB[:].indirect(T.RY[:]), F_.Copy, ["TAB0", "TAB%d" % M, "TAB%d" % C, "RY"], ["SEG"])
        act(T.CH[:, end16], T.SG[:], F_.Identity, ["SG", "RP4"], ["CH"], bias=ch_b, scale=float(C // 2))
        cp(T.H[:, SPARE:SPARE + C].indirect(rk[:]), T.JB[:], ["JB", "RK%d" % t], ["H"])
        scan(T.ZJ[:], T.JB[:], T.SEG[:], -float(MARK), A.max, A.min, ["JB", "SEG"], ["ZJ"])
        if t == 0:
            for b in range(4):
                times("s", T.WIN[:, 2 * b * C:(2 * b + 1) * C], T.X[:, b:4 * C:4], 64.0, ["X0", "X1"], ["WT%d_0" % b, "WT%d_1" % b])
        if t > 0:
            for b in range(2, 4):
                unpack(b)

        cp(T.ZQ[:].indirect(lk[:]), T.ZJ[:], ["ZJ", "LK%d" % t], ["ZQ"])
        between(0)
        ts(T.FG[:], T.ZQ[:], -float(MARK // 2), None, A.is_gt, None, ["ZQ"], ["FG"])
        scan(T.VZ[:], T.ZQ[:], T.CZ[:], -4096.0, A.max, A.add, ["ZQ", "CZ"], ["VZ"])
        scan(T.CU[:], T.FG[:], T.TAB[:, C:2 * C], float(SPARE - 1 - MARK), A.add, A.min, ["FG", "TAB%d" % C], ["CU"])
        between(1)
        scan(T.VC[:], T.CU[:], T.C0[:], -4096.0, A.max, A.add, ["CU", "C0"], ["VC"])
        between(2)
        ts(T.T1[:], T.VC[:, end16], T.SM[:, 2:3], float(L), A.is_ge, A.mult, ["VC", "thr"], ["T1"])
        tt(T.T2[:], T.VC[:, end16], T.VZ[:, end16], A.min, ["VC", "VZ"], ["T2"])
        between(3)
        tt(T.T3[:], T.T1[:], T.T2[:], A.add, ["T1", "T2"], ["T3"])
        ts(T.POS[:], T.T3[:], pos_b, None, A.subtract, None, ["T3", "RP2"], ["POS"])
        cp(T.H[:].indirect(T.POS[:]), T.ZQ[:], ["ZQ", "POS"], ["H"])
        for h in range(2):
            scan(half(T.VH, h), half(T.H, h, SPARE), half(T.CH, h), -4096.0, A.max, A.add, ["H", "CH"], ["VH%d" % h])
        for h in range(2):
            ts(T.OFF[:, h * KH:(h + 1) * KH], T.VH[:, h * MID + 15:(h + 1) * MID:16], off_b, None, A.subtract, None, ["VH%d" % h, "RP3"], ["OFF%d" % h])

        def gather(q, b, h):
            times(q, plane(T.F, b, h), T.WIN[:, 2 * b * C:(2 * b + 2) * C].indirect(T.OFF[:, h * KH:(h + 1) * KH]), 0.015625,
                  ["WT%d_0" % b, "WT%d_1" % b, "WD%d" % b, "OFF%d" % h], ["F%d_%d" % (b, h)])

        def layer(h):
            quant(half(T.FQ, h), half(T.FS, h), words(T.F, h), ["F%d_%d" % (b, h) for b in range(4)], ["FQ%d" % h])
            for b in range(4):
                mm("B%d" % (4 * h + b), T.WQ[:, 128 * b:128 * b + 128], T.WS[:, 128 * b:128 * b + 128], half(T.FQ, h), half(T.FS, h),
                   ["WQ", "WS", "FQ%d" % h], MID)

        def widen(q, h):
            times(q, words(T.F64, h), words(T.F, h), 64.0, ["F%d_%d" % (b, h) for b in range(4)], ["G%d" % h])

        def add(b, h):
            tt(half(T.WIN, h, 2 * b * C), T["B%d" % (4 * h + b)][:, 0:MID], plane(T.F64, b, h), A.add, ["B%d" % (4 * h + b), "G%d" % h], ["WT%d_%d" % (b, h)])

        def scale(q, b, h):
            times(q, plane(T.TT, b, h), half(T.WIN, h, 2 * b * C), 0.015625, ["WT%d_%d" % (b, h)], ["TT%d_%d" % (b, h)])

        def state(h):
            quant_state(t + 1, h, T.TT, ["TT%d_%d" % (b, h) for b in range(4)])

        for q, b, h in (("v", 0, 0), ("v", 1, 0), ("s", 2, 0), ("s", 3, 0), ("s", 2, 1), ("s", 3, 1), ("s", 1, 1)):
            gather(q, b, h)
        layer(0)
        gather("v", 0, 1)
        widen("v", 0)
        layer(1)
        widen("s", 1)
        for h in range(2):
            for b in range(4):
                add(b, h)
                if b < 3:
                    scale("s", b, h)
                if (b, h) == (0, 1):
                    scale("v", 3, 0)
        state(0)
        scale("v", 3, 1)
        state(1)

    tq, tsc, kq = T["TQ%d" % R], T["TS%d" % R], ["TQ%d_0" % R, "TQ%d_1" % R]
    act(T.OT[:], T.H[:, SPARE:SPARE + C], F_.Identity, ["H"], ["OT"], bias=float(MID))
    for h in range(2):
        mm("B%d" % h, T.VQ[:], T.VS[:], half(tq, h), half(tsc, h), ["VQ", kq[h]], MID)
    for h in range(2):
        dma("y", words(T.oc, h), half(tq, h).bitcast(u8), [kq[h]], [])
    dma("s", T.ot[:], T.OT[0:128:16, :], ["OT"], [])
    for k in range(4):
        dma("s", T.osc[4 * k:4 * k + 4, :], tsc[32 * k:32 * k + 4, :], kq, [])
    for h in range(2):
        cp(half(T.Y, h), T["B%d" % h][:, 0:MID], ["B%d" % h], ["Y%d" % h])
        dma("y", half(T.y, h), half(T.Y, h), ["Y%d" % h], [])
    for s, n in count.items():
        if known["g"].get(s, 0) < n:
            g.wait_ge(T.sem[s], n)
